import numpy as np
import ml_dtypes


def mxq(x, axis, fmt="e4m3"):
    dtype, down = {"e4m3": (ml_dtypes.float8_e4m3fn, 7), "e5m2": (ml_dtypes.float8_e5m2, 14)}[fmt]
    v = np.moveaxis(np.asarray(x, np.float32).astype(ml_dtypes.bfloat16).astype(np.float64), axis, -1)
    blocks = v.reshape(v.shape[:-1] + (-1, 32))
    amax = np.abs(blocks).max(-1, keepdims=True)
    byte = np.maximum(np.where(amax > 0, np.frexp(amax)[1] - 1 + 127, 0) - down, 1)
    scale = np.exp2(byte - 127.0)
    codes = (blocks / scale).astype(np.float32).astype(dtype).astype(np.float64)
    return np.moveaxis((codes * scale).reshape(v.shape), -1, axis)


WIDE = False


def mx_kscale(k):
    if not WIDE:
        return np.ones(k)
    levels = np.array([10, -10, 5, -5, 0])
    if k % 512:
        return np.exp2(np.random.permutation(np.resize(levels, k // 32))).repeat(32)
    a = np.empty((k // 512, 16))
    for p in range(k // 512):
        a[p, :8] = np.random.permutation(np.resize(levels, 8))
        for g in range(8):
            far = levels[np.abs(levels - a[p, g]) >= 10]
            a[p, g + 8] = far[np.random.randint(len(far))]
    return np.exp2(a.ravel()).repeat(32)


def f64(x):
    return np.asarray(x).astype(np.float64)


def striped(idx):
    return np.tile(idx.reshape(-1, 16).T, (8, 1)).astype(np.uint16)


def unstriped(offs):
    return offs[:16].T.reshape(-1).astype(np.int64)


E2M1 = np.array([0.0, 0.5, 1.0, 1.5, 2.0, 3.0, 4.0, 6.0, -0.0, -0.5, -1.0, -1.5, -2.0, -3.0, -4.0, -6.0])


def pack_weight(w, fmt):
    k, n = w.shape
    w = f64(np.asarray(w, np.float32).astype(ml_dtypes.bfloat16)).reshape(k // 32, 32, n)
    amax = np.abs(w).max(1)
    if fmt == "e4m3":
        byte = np.frexp(amax)[1] - 1 + 127 - 7
    else:
        mant, ex = np.frexp(amax / 6.0)
        byte = np.where(mant > 0.5, ex, ex - 1) + 127
    byte = np.clip(np.where(amax > 0, byte, 1), 1, 254)
    scaled = (w * np.exp2(127.0 - byte)[:, None, :]).reshape(k, n).astype(np.float32)
    by_word = np.ascontiguousarray(scaled.reshape(k // 512, 128, 4, n).transpose(0, 1, 3, 2))
    if fmt == "e4m3":
        words = by_word.astype(ml_dtypes.float8_e4m3fn).view(np.uint8)
    else:
        c = by_word.astype(ml_dtypes.float4_e2m1fn).view(np.uint8) & 0xF
        words = (c[..., 0::2] | (c[..., 1::2] << 4)).reshape(k // 512, 128, 2 * n)
    return np.ascontiguousarray(words), np.ascontiguousarray(byte.astype(np.uint8).reshape(k // 512, 16, n))


def unpack_weight(words, scales, fmt):
    g, _, n = scales.shape
    words = np.ascontiguousarray(words).reshape(g, 128, n, -1)
    if fmt == "e4m3":
        vals = words.view(ml_dtypes.float8_e4m3fn).astype(np.float64)
    else:
        nib = np.empty((g, 128, n, 4), np.uint8)
        nib[..., 0::2] = words & 0xF
        nib[..., 1::2] = words >> 4
        vals = E2M1[nib]
    vals = vals * np.repeat(np.exp2(scales.astype(np.float64) - 127.0), 8, axis=1)[..., None]
    return vals.transpose(0, 1, 3, 2).reshape(g * 512, n)


def planes(y):
    n, m = y.shape
    v = y.astype(np.float32).astype(ml_dtypes.bfloat16).astype(np.float64).reshape(n // 32, 32, m)
    top = np.abs(v).max(1)
    byte = np.clip(np.where(top > 0, np.frexp(top)[1] - 1 + 127 - 7, 1), 1, 254)
    codes = (v * np.exp2(127.0 - byte)[:, None, :]).reshape(n, m).astype(np.float32).astype(ml_dtypes.float8_e4m3fn).view(np.uint8)
    words = codes.reshape(n // 512, 128, 4, m).transpose(0, 1, 3, 2)
    return np.ascontiguousarray(words), np.ascontiguousarray(byte.astype(np.uint8).reshape(n // 512, 16, m))


def relu(v):
    return np.maximum(v, 0.0)


K, T, E, C, H, N = 512, 768, 6, 256, 512, 512


def by_expert(wq, xq):
    return np.concatenate([wq[e].T @ xq[:, e * C:(e + 1) * C] for e in range(E)], axis=1)


def setup_inputs():
    n = np.random.standard_normal
    s = mx_kscale(K)
    u = mx_kscale(H)
    slot_token = np.concatenate([np.random.permutation(T)[:C] for e in range(E)])
    x = pack_weight(n((K, T)) * s[:, None], "e4m3")
    w = [pack_weight(m, "e2m1") for m in n((E, K, N)) / np.sqrt(K) / s[None, :, None]]
    wa = [pack_weight(m, "e4m3") for m in n((E, K, H)) / np.sqrt(K) / s[None, :, None] * u]
    return {
        "x_words": x[0],
        "x_scales": x[1],
        "w_words": np.stack([m[0] for m in w]),
        "w_scales": np.stack([m[1] for m in w]),
        "wa_words": np.stack([m[0] for m in wa]),
        "wa_scales": np.stack([m[1] for m in wa]),
        "wb": (n((E, H, N)) / np.sqrt(H) / u[None, :, None]).astype(np.float32),
        "offs": striped(slot_token),
    }


def reference(x_words, x_scales, w_words, w_scales, wa_words, wa_scales, wb, offs):
    w = np.stack([unpack_weight(w_words[e], w_scales[e], "e2m1") for e in range(E)])
    wa = np.stack([unpack_weight(wa_words[e], wa_scales[e], "e4m3") for e in range(E)])
    wbq = mxq(f64(wb), 1, "e4m3")
    idx = unstriped(offs)
    xq = unpack_weight(x_words, x_scales, "e4m3")[:, idx]
    h = relu(by_expert(wa, xq))
    y = by_expert(w, xq) + by_expert(wbq, mxq(h, 0, "e4m3"))
    out = y
    out_0 = out
    return (out_0,) + planes(out_0)

@@ -1,0 +1,238 @@
+from contextlib import ExitStack
+
+import concourse.mybir as mybir
+
+K, T, E, C, H, N = 512, 768, 6, 256, 512, 512
+FLOPS = 3 * 2 * 512 * 512 * E * C
+
+F32 = mybir.dt.float32
+BF16 = mybir.dt.bfloat16
+I32 = mybir.dt.int32
+U32 = mybir.dt.uint32
+U16 = mybir.dt.uint16
+U8 = mybir.dt.uint8
+FP8X4 = mybir.dt.float8_e4m3fn_x4
+FP4X4 = mybir.dt.float4_e2m1fn_x4
+RELU = mybir.ActivationFunctionType.Relu
+
+P = 128
+PACK = 4
+HALF = 128
+WA_ROW = 4
+VECTOR_ROUNDS = [(2, 1), (4, 1)]
+
+
+def tile_moe_elr_s_relu_kernel(
+    tc, x_words, x_scales, w_words, w_scales, wa_words, wa_scales, wb, offs, out_0, out_1, out_2
+):
+    nc = tc.nc
+    with ExitStack() as ctx:
+        keep = ctx.enter_context(tc.tile_pool(name="keep", bufs=1))
+        ring = ctx.enter_context(tc.tile_pool(name="ring", bufs=3))
+        psum = ctx.enter_context(tc.psum_pool(name="psum", bufs=4))
+
+        offsets = keep.tile([P, E * C // 16], U16, name="offsets")
+        xw = keep.tile([P, T], U32, name="xw", align_bytes=64)
+        xs = keep.tile([P, T], U8, name="xs", align_bytes=64)
+        sc_raw = keep.tile([P, E, N], U8, name="sc_raw", align_bytes=64)
+        wb_first = [keep.tile([P, PACK, N // 2], F32, name="wb_first%d" % u, align_bytes=64) for u in range(2)]
+        wb_raw = [None] + [keep.tile([P, PACK, N], F32, name="wb_raw%d" % e, align_bytes=64) for e in range(1, E)]
+        wa_raw = [keep.tile([P, H], I32, name="wa_raw%d" % e, align_bytes=64) for e in range(E)]
+        w_raw = [keep.tile([P, 2 * N], U8, name="w_raw%d" % e, align_bytes=64) for e in range(E)]
+        y_scales = keep.tile([P, E * C], U8, name="y_scales", align_bytes=64)
+
+        nc.gpsimd.memset(sc_raw[:].rearrange("p e n -> p (e n)").bitcast(I32), 0)
+
+        def wb_rows(e):
+            return wb[e].rearrange("(p j) n -> p j n", j=PACK)
+
+        def load_wa(e):
+            nc.sync.dma_start(out=wa_raw[e][:], in_=wa_words[e, 0].rearrange("p n d -> p (n d)").bitcast(I32))
+
+        def load_w(e):
+            nc.sync.dma_start(out=w_raw[e][:].bitcast(I32), in_=w_words[e, 0].bitcast(I32))
+
+        def load_scale_rows(row, scales, q):
+            nc.sync.dma_start(
+                out=sc_raw[32 * q + row : 32 * q + row + 4, :, :].bitcast(I32),
+                in_=scales[:, 0, 4 * q : 4 * q + 4, :].rearrange("e r n -> r e n").bitcast(I32),
+            )
+
+        nc.sync.dma_start(offsets[:], offs)
+        for q in range(4):
+            rows = x_scales[0, 4 * q : 4 * q + 4, :].bitcast(I32)
+            nc.sync.dma_start(out=xs[32 * q : 32 * q + 32, :].bitcast(I32), in_=rows.unsqueeze(0).to_broadcast([8, 4, T // 4]))
+        nc.sync.dma_start(out=xw[:].bitcast(I32), in_=x_words[0].rearrange("p t d -> p (t d)").bitcast(I32))
+        nc.sync.dma_start(out=wb_first[0][:], in_=wb_rows(0)[:, :, : N // 2])
+        load_wa(0)
+        for q in range(4):
+            load_scale_rows(WA_ROW, wa_scales, q)
+        nc.sync.dma_start(out=wb_first[1][:], in_=wb_rows(0)[:, :, N // 2 :])
+        for q in range(4):
+            load_scale_rows(0, w_scales, q)
+        load_w(0)
+        for e in range(1, E):
+            load_wa(e)
+            nc.sync.dma_start(out=wb_raw[e][:], in_=wb_rows(e))
+            load_w(e)
+
+        tok = {}
+
+        def gather(e):
+            words = ring.tile([P, C], U32, name="xg_words", align_bytes=64)
+            scales = ring.tile([P, C], U8, name="xg_scales", align_bytes=64)
+            lst = offsets[:, e * C // 16 : (e + 1) * C // 16]
+            nc.vector.tensor_copy(words[:], xw[:].indirect(lst))
+            nc.vector.tensor_copy(scales[:], xs[:].indirect(lst))
+            tok[e] = (words, scales, 0)
+
+        st = {}
+
+        def deal(e):
+            wa_p = ring.tile([P, H], I32, name="wa_p", align_bytes=64)
+            sc_p = ring.tile([P, N], U8, name="sc_p", align_bytes=64)
+            w_p = ring.tile([P, 2 * N], U8, name="w_p", align_bytes=64)
+            nc.vector.tensor_copy(
+                out=wa_p[:].rearrange("p (t m) -> p m t", t=PACK), in_=wa_raw[e][:].rearrange("p (m t) -> p m t", t=PACK)
+            )
+            nc.vector.tensor_copy(
+                out=sc_p[:].rearrange("p (t m) -> p t m", t=PACK), in_=sc_raw[:, e, :].rearrange("p (m t) -> p t m", t=PACK)
+            )
+            nc.vector.tensor_copy(
+                out=w_p[:].bitcast(U16).rearrange("p (t m) -> p t m", t=PACK),
+                in_=w_raw[e][:].bitcast(U16).rearrange("p (m t) -> p t m", t=PACK),
+            )
+            st[e, "wa"], st[e, "sc"], st[e, "w"] = wa_p, sc_p, w_p
+
+        def round_wb(e):
+            wb_bf = ring.tile([P, PACK, P, PACK], BF16, name="wb_bf", align_bytes=64)
+            for u in range(2):
+                dst = wb_bf[:, :, u * 64 : (u + 1) * 64, :].rearrange("p t m j -> p m t j")
+                half = wb_first[u][:] if e == 0 else wb_raw[e][:, :, u * (N // 2) : (u + 1) * (N // 2)]
+                src = half.rearrange("p j (m t) -> p m t j", t=PACK)
+                if (e, u) in VECTOR_ROUNDS:
+                    nc.vector.tensor_copy(out=dst, in_=src)
+                else:
+                    nc.scalar.copy(out=dst, in_=src)
+            st[e, "wb_bf"] = wb_bf
+
+        def quant_wb(e):
+            words = ring.tile([P, N], U32, name="wb_words", align_bytes=64)
+            scales = ring.tile([P, N], U8, name="wb_scales", align_bytes=64)
+            nc.vector.quantize_mx(
+                out=words[:].bitcast(FP8X4), scales=scales[:], in_=st[e, "wb_bf"][:].rearrange("p t m j -> p (t m j)")
+            )
+            st[e, "wbq"] = (words, scales)
+
+        def hidden(e):
+            xg_w, xg_s, c0 = tok[e]
+            h_bf = ring.tile([P, C, PACK], BF16, name="h_bf", align_bytes=64)
+            for u in range(C // HALF):
+                cols = slice(c0 + u * HALF, c0 + (u + 1) * HALF)
+                bank = psum.tile([P, PACK, HALF], F32, name="h_bank")
+                for t in range(PACK):
+                    m = slice(t * P, (t + 1) * P)
+                    nc.tensor.matmul_mx(
+                        out=bank[:, t, :],
+                        lhsT=st[e, "wa"][:, m].bitcast(FP8X4),
+                        lhsT_scale=st[e, "sc"][WA_ROW:P, m],
+                        rhs=xg_w[:, cols].bitcast(FP8X4),
+                        rhs_scale=xg_s[:, cols],
+                        start=True,
+                        stop=True,
+                    )
+                nc.scalar.activation(
+                    out=h_bf[:, u * HALF : (u + 1) * HALF, :], in_=bank[:].rearrange("p t s -> p s t"), func=RELU
+                )
+            st[e, "h_bf"] = h_bf
+
+        def quant_h(e):
+            words = ring.tile([P, C], U32, name="h_words", align_bytes=64)
+            scales = ring.tile([P, C], U8, name="h_scales", align_bytes=64)
+            nc.vector.quantize_mx(
+                out=words[:].bitcast(FP8X4), scales=scales[:], in_=st[e, "h_bf"][:].rearrange("p s t -> p (s t)")
+            )
+            st[e, "hq"] = (words, scales)
+
+        rows_out = out_0.rearrange("(p t) s -> p t s", t=PACK)
+        words_out = out_1[0].rearrange("p s d -> p (s d)")
+
+        def result(e):
+            xg_w, xg_s, c0 = tok[e]
+            wb_w, wb_s = st[e, "wbq"]
+            h_w, h_s = st[e, "hq"]
+            y = keep.tile([P, PACK, C], F32, name="y%d" % e, align_bytes=64)
+            for u in range(C // HALF):
+                cols = slice(c0 + u * HALF, c0 + (u + 1) * HALF)
+                own = slice(u * HALF, (u + 1) * HALF)
+                bank = psum.tile([P, PACK, HALF], F32, name="y_bank")
+                for t in range(PACK):
+                    m = slice(t * P, (t + 1) * P)
+                    nc.tensor.matmul_mx(
+                        out=bank[:, t, :],
+                        lhsT=st[e, "w"][:, 2 * t * P : 2 * (t + 1) * P].bitcast(FP4X4),
+                        lhsT_scale=st[e, "sc"][:, m],
+                        rhs=xg_w[:, cols].bitcast(FP8X4),
+                        rhs_scale=xg_s[:, cols],
+                        start=True,
+                        stop=False,
+                    )
+                    nc.tensor.matmul_mx(
+                        out=bank[:, t, :],
+                        lhsT=wb_w[:, m].bitcast(FP8X4),
+                        lhsT_scale=wb_s[:, m],
+                        rhs=h_w[:, own].bitcast(FP8X4),
+                        rhs_scale=h_s[:, own],
+                        start=False,
+                        stop=True,
+                    )
+                nc.scalar.copy(out=y[:, :, own], in_=bank[:])
+                if e == E - 1:
+                    nc.sync.dma_start(out=rows_out[:, :, e * C + u * HALF : e * C + (u + 1) * HALF], in_=y[:, :, own])
+            if e < E - 1:
+                nc.sync.dma_start(out=rows_out[:, :, e * C : (e + 1) * C], in_=y[:])
+            st[e, "y"] = y
+
+        def round_y(e, c0, c1):
+            y_bf = ring.tile([P, (c1 - c0) * PACK], BF16, name="y_bf", align_bytes=64)
+            nc.vector.tensor_copy(
+                out=y_bf[:].rearrange("p (c i t) -> p c t i", i=4, t=PACK),
+                in_=st[e, "y"][:, :, c0:c1].rearrange("p t (c i) -> p c t i", i=4),
+            )
+            st[e, "y_bf", c0] = y_bf
+
+        def quant_y(e, c0, c1):
+            words = keep.tile([P, c1 - c0], U32, name="y_words%d_%d" % (e, c0), align_bytes=64)
+            nc.vector.quantize_mx(
+                out=words[:].bitcast(FP8X4), scales=y_scales[:, e * C + c0 : e * C + c1], in_=st[e, "y_bf", c0][:]
+            )
+            nc.sync.dma_start(out=words_out[:, 4 * (e * C + c0) : 4 * (e * C + c1)].bitcast(I32), in_=words[:].bitcast(I32))
+
+        gather(0)
+        round_wb(0)
+        gather(1)
+        for s in range(E + 1):
+            if s < E:
+                deal(s)
+                hidden(s)
+                quant_wb(s)
+            if s >= 2:
+                quant_y(s - 2, 0, C)
+            if s >= 1:
+                result(s - 1)
+            if s < E:
+                quant_h(s)
+            if s + 1 < E:
+                round_wb(s + 1)
+            if s + 2 < E:
+                gather(s + 2)
+            if 1 <= s < E:
+                round_y(s - 1, 0, C)
+        for u in range(2):
+            round_y(E - 1, u * HALF, (u + 1) * HALF)
+        for u in range(2):
+            quant_y(E - 1, u * HALF, (u + 1) * HALF)
+        for q in range(4):
+            nc.sync.dma_start(
+                out=out_2[0, 4 * q : 4 * q + 4, :].bitcast(I32), in_=y_scales[32 * q : 32 * q + 4, :].bitcast(I32)
+            )

@@ -19,7 +19,8 @@ P = 128
 PACK = 4
 HALF = 128
 WA_ROW = 4
-VECTOR_ROUNDS = [(2, 1), (4, 1)]
+VECTOR_FROM = 2
+SPLIT_LOADS = 2
 
 
 def tile_moe_elr_s_relu_kernel(
@@ -35,10 +36,18 @@ def tile_moe_elr_s_relu_kernel(
         xw = keep.tile([P, T], U32, name="xw", align_bytes=64)
         xs = keep.tile([P, T], U8, name="xs", align_bytes=64)
         sc_raw = keep.tile([P, E, N], U8, name="sc_raw", align_bytes=64)
-        wb_first = [keep.tile([P, PACK, N // 2], F32, name="wb_first%d" % u, align_bytes=64) for u in range(2)]
-        wb_raw = [None] + [keep.tile([P, PACK, N], F32, name="wb_raw%d" % e, align_bytes=64) for e in range(1, E)]
+        wb_half = {}
+        for e in range(E):
+            if e < SPLIT_LOADS:
+                for u in range(2):
+                    wb_half[e, u] = keep.tile([P, PACK, N // 2], F32, name="wb_raw%d_%d" % (e, u), align_bytes=64)[:]
+            else:
+                wb_half[e] = keep.tile([P, PACK, N], F32, name="wb_raw%d" % e, align_bytes=64)
+                for u in range(2):
+                    wb_half[e, u] = wb_half[e][:, :, u * (N // 2) : (u + 1) * (N // 2)]
         wa_raw = [keep.tile([P, H], I32, name="wa_raw%d" % e, align_bytes=64) for e in range(E)]
         w_raw = [keep.tile([P, 2 * N], U8, name="w_raw%d" % e, align_bytes=64) for e in range(E)]
+        y_words = keep.tile([P, E * C], U32, name="y_words", align_bytes=64)
         y_scales = keep.tile([P, E * C], U8, name="y_scales", align_bytes=64)
 
         nc.gpsimd.memset(sc_raw[:].rearrange("p e n -> p (e n)").bitcast(I32), 0)
@@ -52,65 +61,70 @@ def tile_moe_elr_s_relu_kernel(
         def load_w(e):
             nc.sync.dma_start(out=w_raw[e][:].bitcast(I32), in_=w_words[e, 0].bitcast(I32))
 
-        def load_scale_rows(row, scales, q):
-            nc.sync.dma_start(
-                out=sc_raw[32 * q + row : 32 * q + row + 4, :, :].bitcast(I32),
-                in_=scales[:, 0, 4 * q : 4 * q + 4, :].rearrange("e r n -> r e n").bitcast(I32),
-            )
+        def load_wb_half(e, u):
+            nc.sync.dma_start(out=wb_half[e, u], in_=wb_rows(e)[:, :, u * (N // 2) : (u + 1) * (N // 2)])
+
+        def load_scale_rows(row, scales):
+            by_row = scales[:, 0].rearrange("e (q r) n -> r q e n", r=4)
+            for r in range(4):
+                nc.sync.dma_start(out=sc_raw[row + r : P : 32, :, :].bitcast(I32), in_=by_row[r].bitcast(I32))
 
         nc.sync.dma_start(offsets[:], offs)
         for q in range(4):
             rows = x_scales[0, 4 * q : 4 * q + 4, :].bitcast(I32)
             nc.sync.dma_start(out=xs[32 * q : 32 * q + 32, :].bitcast(I32), in_=rows.unsqueeze(0).to_broadcast([8, 4, T // 4]))
+        load_wb_half(0, 0)
         nc.sync.dma_start(out=xw[:].bitcast(I32), in_=x_words[0].rearrange("p t d -> p (t d)").bitcast(I32))
-        nc.sync.dma_start(out=wb_first[0][:], in_=wb_rows(0)[:, :, : N // 2])
+        load_wb_half(0, 1)
+        load_scale_rows(WA_ROW, wa_scales)
+        load_wb_half(1, 0)
         load_wa(0)
-        for q in range(4):
-            load_scale_rows(WA_ROW, wa_scales, q)
-        nc.sync.dma_start(out=wb_first[1][:], in_=wb_rows(0)[:, :, N // 2 :])
-        for q in range(4):
-            load_scale_rows(0, w_scales, q)
+        load_scale_rows(0, w_scales)
+        load_wb_half(1, 1)
         load_w(0)
         for e in range(1, E):
             load_wa(e)
-            nc.sync.dma_start(out=wb_raw[e][:], in_=wb_rows(e))
             load_w(e)
+            if e + 1 < E:
+                nc.sync.dma_start(out=wb_half[e + 1][:], in_=wb_rows(e + 1))
 
         tok = {}
+        st = {}
+
+        def gather_scales(pair):
+            scales = keep.tile([P, 2 * C], U8, name="xg_scales%d" % pair, align_bytes=64)
+            nc.vector.tensor_copy(scales[:], xs[:].indirect(offsets[:, pair * C // 8 : (pair + 1) * C // 8]))
+            st[pair, "xg_scales"] = scales
 
         def gather(e):
             words = ring.tile([P, C], U32, name="xg_words", align_bytes=64)
-            scales = ring.tile([P, C], U8, name="xg_scales", align_bytes=64)
-            lst = offsets[:, e * C // 16 : (e + 1) * C // 16]
-            nc.vector.tensor_copy(words[:], xw[:].indirect(lst))
-            nc.vector.tensor_copy(scales[:], xs[:].indirect(lst))
-            tok[e] = (words, scales, 0)
-
-        st = {}
+            nc.vector.tensor_copy(words[:], xw[:].indirect(offsets[:, e * C // 16 : (e + 1) * C // 16]))
+            tok[e] = (words, st[e // 2, "xg_scales"], (e % 2) * C)
 
         def deal(e):
             wa_p = ring.tile([P, H], I32, name="wa_p", align_bytes=64)
-            sc_p = ring.tile([P, N], U8, name="sc_p", align_bytes=64)
             w_p = ring.tile([P, 2 * N], U8, name="w_p", align_bytes=64)
             nc.vector.tensor_copy(
                 out=wa_p[:].rearrange("p (t m) -> p m t", t=PACK), in_=wa_raw[e][:].rearrange("p (m t) -> p m t", t=PACK)
             )
-            nc.vector.tensor_copy(
-                out=sc_p[:].rearrange("p (t m) -> p t m", t=PACK), in_=sc_raw[:, e, :].rearrange("p (m t) -> p t m", t=PACK)
-            )
+            if e % 2 == 0:
+                st["sc_pair"] = ring.tile([P, 2, N], U8, name="sc_p", align_bytes=64, bufs=2)
+                nc.vector.tensor_copy(
+                    out=st["sc_pair"][:].rearrange("p e (t m) -> p e t m", t=PACK),
+                    in_=sc_raw[:, e : e + 2, :].rearrange("p e (m t) -> p e t m", t=PACK),
+                )
             nc.vector.tensor_copy(
                 out=w_p[:].bitcast(U16).rearrange("p (t m) -> p t m", t=PACK),
                 in_=w_raw[e][:].bitcast(U16).rearrange("p (m t) -> p t m", t=PACK),
             )
-            st[e, "wa"], st[e, "sc"], st[e, "w"] = wa_p, sc_p, w_p
+            st[e, "wa"], st[e, "sc"], st[e, "w"] = wa_p, st["sc_pair"], w_p
 
         def round_wb(e):
             wb_bf = ring.tile([P, PACK, P, PACK], BF16, name="wb_bf", align_bytes=64)
             for u in range(2):
-                dst = wb_bf[:, :, u * 64 : (u + 1) * 64, :].rearrange("p t m j -> p m t j")
-                half = wb_first[u][:] if e == 0 else wb_raw[e][:, :, u * (N // 2) : (u + 1) * (N // 2)]
-                src = half.rearrange("p j (m t) -> p m t j", t=PACK)
-                if (e, u) in VECTOR_ROUNDS:
+                dst = wb_bf[:, :, u * 64 : (u + 1) * 64, :].rearrange("p t m j -> p m j t")
+                src = wb_half[e, u].rearrange("p j (m t) -> p m j t", t=PACK)
+                if u == 1 and e >= VECTOR_FROM:
                     nc.vector.tensor_copy(out=dst, in_=src)
                 else:
                     nc.scalar.copy(out=dst, in_=src)
@@ -135,8 +149,8 @@ def tile_moe_elr_s_relu_kernel(
                     nc.tensor.matmul_mx(
                         out=bank[:, t, :],
                         lhsT=st[e, "wa"][:, m].bitcast(FP8X4),
-                        lhsT_scale=st[e, "sc"][WA_ROW:P, m],
-                        rhs=xg_w[:, cols].bitcast(FP8X4),
+                        lhsT_scale=st[e, "sc"][WA_ROW:P, e % 2, m],
+                        rhs=xg_w[:, u * HALF : (u + 1) * HALF].bitcast(FP8X4),
                         rhs_scale=xg_s[:, cols],
                         start=True,
                         stop=True,
@@ -149,9 +163,14 @@ def tile_moe_elr_s_relu_kernel(
         def quant_h(e):
             words = ring.tile([P, C], U32, name="h_words", align_bytes=64)
             scales = ring.tile([P, C], U8, name="h_scales", align_bytes=64)
-            nc.vector.quantize_mx(
-                out=words[:].bitcast(FP8X4), scales=scales[:], in_=st[e, "h_bf"][:].rearrange("p s t -> p (s t)")
-            )
+            width = HALF if e == E - 1 else C
+            for c0 in range(0, C, width):
+                cols = slice(c0, c0 + width)
+                nc.vector.quantize_mx(
+                    out=words[:, cols].bitcast(FP8X4),
+                    scales=scales[:, cols],
+                    in_=st[e, "h_bf"][:, cols, :].rearrange("p s t -> p (s t)"),
+                )
             st[e, "hq"] = (words, scales)
 
         rows_out = out_0.rearrange("(p t) s -> p t s", t=PACK)
@@ -171,8 +190,8 @@ def tile_moe_elr_s_relu_kernel(
                     nc.tensor.matmul_mx(
                         out=bank[:, t, :],
                         lhsT=st[e, "w"][:, 2 * t * P : 2 * (t + 1) * P].bitcast(FP4X4),
-                        lhsT_scale=st[e, "sc"][:, m],
-                        rhs=xg_w[:, cols].bitcast(FP8X4),
+                        lhsT_scale=st[e, "sc"][:, e % 2, m],
+                        rhs=xg_w[:, u * HALF : (u + 1) * HALF].bitcast(FP8X4),
                         rhs_scale=xg_s[:, cols],
                         start=True,
                         stop=False,
@@ -186,6 +205,12 @@ def tile_moe_elr_s_relu_kernel(
                         start=False,
                         stop=True,
                     )
+                if (e, u) == (E - 1, 1):
+                    y_bf = ring.tile([P, HALF * PACK], BF16, name="y_bf", align_bytes=64)
+                    nc.vector.tensor_copy(
+                        out=y_bf[:].rearrange("p (s t) -> p s t", t=PACK), in_=bank[:].rearrange("p t s -> p s t")
+                    )
+                    st[e, "y_bf", HALF] = y_bf
                 nc.scalar.copy(out=y[:, :, own], in_=bank[:])
                 if e == E - 1:
                     nc.sync.dma_start(out=rows_out[:, :, e * C + u * HALF : e * C + (u + 1) * HALF], in_=y[:, :, own])
@@ -202,37 +227,42 @@ def tile_moe_elr_s_relu_kernel(
             st[e, "y_bf", c0] = y_bf
 
         def quant_y(e, c0, c1):
-            words = keep.tile([P, c1 - c0], U32, name="y_words%d_%d" % (e, c0), align_bytes=64)
             nc.vector.quantize_mx(
-                out=words[:].bitcast(FP8X4), scales=y_scales[:, e * C + c0 : e * C + c1], in_=st[e, "y_bf", c0][:]
+                out=y_words[:, e * C + c0 : e * C + c1].bitcast(FP8X4),
+                scales=y_scales[:, e * C + c0 : e * C + c1],
+                in_=st[e, "y_bf", c0][:],
             )
-            nc.sync.dma_start(out=words_out[:, 4 * (e * C + c0) : 4 * (e * C + c1)].bitcast(I32), in_=words[:].bitcast(I32))
 
+        def store_words(s0, s1):
+            nc.sync.dma_start(out=words_out[:, 4 * s0 : 4 * s1].bitcast(I32), in_=y_words[:, s0:s1].bitcast(I32))
+
+        for pair in range(E // 2):
+            gather_scales(pair)
         gather(0)
         round_wb(0)
         gather(1)
-        for s in range(E + 1):
-            if s < E:
-                deal(s)
-                hidden(s)
-                quant_wb(s)
-            if s >= 2:
-                quant_y(s - 2, 0, C)
-            if s >= 1:
-                result(s - 1)
-            if s < E:
-                quant_h(s)
+        deal(0)
+        hidden(0)
+        for s in range(E):
+            quant_wb(s)
+            quant_h(s)
             if s + 1 < E:
+                deal(s + 1)
+                hidden(s + 1)
                 round_wb(s + 1)
             if s + 2 < E:
                 gather(s + 2)
-            if 1 <= s < E:
-                round_y(s - 1, 0, C)
-        for u in range(2):
-            round_y(E - 1, u * HALF, (u + 1) * HALF)
-        for u in range(2):
-            quant_y(E - 1, u * HALF, (u + 1) * HALF)
-        for q in range(4):
-            nc.sync.dma_start(
-                out=out_2[0, 4 * q : 4 * q + 4, :].bitcast(I32), in_=y_scales[32 * q : 32 * q + 4, :].bitcast(I32)
-            )
+            result(s)
+            if s + 1 < E:
+                round_y(s, 0, C)
+                quant_y(s, 0, C)
+            if s in (1, 3):
+                store_words((s - 1) * C, (s + 1) * C)
+        round_y(E - 1, 0, HALF)
+        quant_y(E - 1, 0, HALF)
+        store_words((E - 2) * C, E * C - HALF)
+        quant_y(E - 1, HALF, C)
+        store_words(E * C - HALF, E * C)
+        by_row = out_2[0].rearrange("(q r) s -> r q s", r=4)
+        for r in range(4):
+            nc.scalar.dma_start(out=by_row[r].bitcast(I32), in_=y_scales[r:P:32, :].bitcast(I32))

@@ -21,6 +21,8 @@ HALF = 128
 WA_ROW = 4
 VECTOR_FROM = 2
 SPLIT_LOADS = 2
+IN_GROUPS = [(0, 1), (1, 3), (3, 5), (5, 6)]
+OUT_GROUPS = [(0, 2), (2, 4), (4, 5), (5, 6)]
 
 
 def tile_moe_elr_s_relu_kernel(
@@ -45,8 +47,8 @@ def tile_moe_elr_s_relu_kernel(
                 wb_half[e] = keep.tile([P, PACK, N], F32, name="wb_raw%d" % e, align_bytes=64)
                 for u in range(2):
                     wb_half[e, u] = wb_half[e][:, :, u * (N // 2) : (u + 1) * (N // 2)]
-        wa_raw = [keep.tile([P, H], I32, name="wa_raw%d" % e, align_bytes=64) for e in range(E)]
-        w_raw = [keep.tile([P, 2 * N], U8, name="w_raw%d" % e, align_bytes=64) for e in range(E)]
+        wa_raw = {e0: keep.tile([P, e1 - e0, H], I32, name="wa_raw%d" % e0, align_bytes=64) for e0, e1 in IN_GROUPS}
+        w_raw = {e0: keep.tile([P, e1 - e0, 2 * N], U8, name="w_raw%d" % e0, align_bytes=64) for e0, e1 in IN_GROUPS}
         y_words = keep.tile([P, E * C], U32, name="y_words", align_bytes=64)
         y_scales = keep.tile([P, E * C], U8, name="y_scales", align_bytes=64)
 
@@ -55,11 +57,11 @@ def tile_moe_elr_s_relu_kernel(
         def wb_rows(e):
             return wb[e].rearrange("(p j) n -> p j n", j=PACK)
 
-        def load_wa(e):
-            nc.sync.dma_start(out=wa_raw[e][:], in_=wa_words[e, 0].rearrange("p n d -> p (n d)").bitcast(I32))
+        def load_wa(e0, e1):
+            nc.sync.dma_start(out=wa_raw[e0][:], in_=wa_words[e0:e1, 0].rearrange("e p n d -> p e (n d)").bitcast(I32))
 
-        def load_w(e):
-            nc.sync.dma_start(out=w_raw[e][:].bitcast(I32), in_=w_words[e, 0].bitcast(I32))
+        def load_w(e0, e1):
+            nc.sync.dma_start(out=w_raw[e0][:].bitcast(I32), in_=w_words[e0:e1, 0].rearrange("e p b -> p e b").bitcast(I32))
 
         def load_wb_half(e, u):
             nc.sync.dma_start(out=wb_half[e, u], in_=wb_rows(e)[:, :, u * (N // 2) : (u + 1) * (N // 2)])
@@ -78,15 +80,15 @@ def tile_moe_elr_s_relu_kernel(
         load_wb_half(0, 1)
         load_scale_rows(WA_ROW, wa_scales)
         load_wb_half(1, 0)
-        load_wa(0)
+        load_wa(0, 1)
         load_scale_rows(0, w_scales)
         load_wb_half(1, 1)
-        load_w(0)
-        for e in range(1, E):
-            load_wa(e)
-            load_w(e)
-            if e + 1 < E:
-                nc.sync.dma_start(out=wb_half[e + 1][:], in_=wb_rows(e + 1))
+        load_w(0, 1)
+        for e0, e1 in IN_GROUPS[1:]:
+            load_wa(e0, e1)
+            load_w(e0, e1)
+            for e in range(e0 + 1, min(e1 + 1, E)):
+                nc.sync.dma_start(out=wb_half[e][:], in_=wb_rows(e))
 
         tok = {}
         st = {}
@@ -96,35 +98,54 @@ def tile_moe_elr_s_relu_kernel(
             nc.vector.tensor_copy(scales[:], xs[:].indirect(offsets[:, pair * C // 8 : (pair + 1) * C // 8]))
             st[pair, "xg_scales"] = scales
 
-        def gather(e):
-            words = ring.tile([P, C], U32, name="xg_words", align_bytes=64)
-            nc.vector.tensor_copy(words[:], xw[:].indirect(offsets[:, e * C // 16 : (e + 1) * C // 16]))
-            tok[e] = (words, st[e // 2, "xg_scales"], (e % 2) * C)
+        def gather(e0, e1):
+            words = ring.tile([P, (e1 - e0) * C], U32, name="xg_words", align_bytes=64, bufs=2)
+            nc.vector.tensor_copy(words[:], xw[:].indirect(offsets[:, e0 * C // 16 : e1 * C // 16]))
+            for e in range(e0, e1):
+                tok[e] = (words[:, (e - e0) * C : (e - e0 + 1) * C], st[e // 2, "xg_scales"], (e % 2) * C)
+
+        def deal_wa(e0, e1):
+            wa_p = ring.tile([P, e1 - e0, H], I32, name="wa_p", align_bytes=64, bufs=2)
+            nc.vector.tensor_copy(
+                out=wa_p[:].rearrange("p e (t m) -> p e m t", t=PACK),
+                in_=wa_raw[e0][:].rearrange("p e (m t) -> p e m t", t=PACK),
+            )
+            for e in range(e0, e1):
+                st[e, "wa"] = wa_p[:, e - e0, :]
+
+        def deal_w(e0, e1):
+            w_p = ring.tile([P, e1 - e0, 2 * N], U8, name="w_p", align_bytes=64, bufs=2)
+            nc.vector.tensor_copy(
+                out=w_p[:].bitcast(U16).rearrange("p e (t m) -> p e t m", t=PACK),
+                in_=w_raw[e0][:].bitcast(U16).rearrange("p e (m t) -> p e t m", t=PACK),
+            )
+            for e in range(e0, e1):
+                st[e, "w"] = w_p[:, e - e0, :]
+
+        def deal_scales(e):
+            sc_p = ring.tile([P, 2, N], U8, name="sc_p", align_bytes=64, bufs=2)
+            nc.vector.tensor_copy(
+                out=sc_p[:].rearrange("p e (t m) -> p e t m", t=PACK),
+                in_=sc_raw[:, e : e + 2, :].rearrange("p e (m t) -> p e t m", t=PACK),
+            )
+            st[e, "sc"] = st[e + 1, "sc"] = sc_p
+
+        in_group = dict(IN_GROUPS)
 
         def deal(e):
-            wa_p = ring.tile([P, H], I32, name="wa_p", align_bytes=64)
-            w_p = ring.tile([P, 2 * N], U8, name="w_p", align_bytes=64)
-            nc.vector.tensor_copy(
-                out=wa_p[:].rearrange("p (t m) -> p m t", t=PACK), in_=wa_raw[e][:].rearrange("p (m t) -> p m t", t=PACK)
-            )
+            if e in in_group:
+                deal_wa(e, in_group[e])
             if e % 2 == 0:
-                st["sc_pair"] = ring.tile([P, 2, N], U8, name="sc_p", align_bytes=64, bufs=2)
-                nc.vector.tensor_copy(
-                    out=st["sc_pair"][:].rearrange("p e (t m) -> p e t m", t=PACK),
-                    in_=sc_raw[:, e : e + 2, :].rearrange("p e (m t) -> p e t m", t=PACK),
-                )
-            nc.vector.tensor_copy(
-                out=w_p[:].bitcast(U16).rearrange("p (t m) -> p t m", t=PACK),
-                in_=w_raw[e][:].bitcast(U16).rearrange("p (m t) -> p t m", t=PACK),
-            )
-            st[e, "wa"], st[e, "sc"], st[e, "w"] = wa_p, st["sc_pair"], w_p
+                deal_scales(e)
+            if e in in_group:
+                deal_w(e, in_group[e])
 
         def round_wb(e):
             wb_bf = ring.tile([P, PACK, P, PACK], BF16, name="wb_bf", align_bytes=64)
             for u in range(2):
                 dst = wb_bf[:, :, u * 64 : (u + 1) * 64, :].rearrange("p t m j -> p m j t")
                 src = wb_half[e, u].rearrange("p j (m t) -> p m j t", t=PACK)
-                if u == 1 and e >= VECTOR_FROM:
+                if (u == 1 and e >= VECTOR_FROM) or e == E - 1:
                     nc.vector.tensor_copy(out=dst, in_=src)
                 else:
                     nc.scalar.copy(out=dst, in_=src)
@@ -176,14 +197,20 @@ def tile_moe_elr_s_relu_kernel(
         rows_out = out_0.rearrange("(p t) s -> p t s", t=PACK)
         words_out = out_1[0].rearrange("p s d -> p (s d)")
 
+        out_group = {e: (e0, e1) for e0, e1 in OUT_GROUPS for e in range(e0, e1)}
+
         def result(e):
             xg_w, xg_s, c0 = tok[e]
             wb_w, wb_s = st[e, "wbq"]
             h_w, h_s = st[e, "hq"]
-            y = keep.tile([P, PACK, C], F32, name="y%d" % e, align_bytes=64)
+            e0, e1 = out_group[e]
+            if e == e0:
+                st[e0, "y"] = keep.tile([P, PACK, (e1 - e0) * C], F32, name="y%d" % e0, align_bytes=64)
+            y = st[e0, "y"]
             for u in range(C // HALF):
                 cols = slice(c0 + u * HALF, c0 + (u + 1) * HALF)
                 own = slice(u * HALF, (u + 1) * HALF)
+                place = slice((e - e0) * C + u * HALF, (e - e0) * C + (u + 1) * HALF)
                 bank = psum.tile([P, PACK, HALF], F32, name="y_bank")
                 for t in range(PACK):
                     m = slice(t * P, (t + 1) * P)
@@ -191,7 +218,7 @@ def tile_moe_elr_s_relu_kernel(
                         out=bank[:, t, :],
                         lhsT=st[e, "w"][:, 2 * t * P : 2 * (t + 1) * P].bitcast(FP4X4),
                         lhsT_scale=st[e, "sc"][:, e % 2, m],
-                        rhs=xg_w[:, u * HALF : (u + 1) * HALF].bitcast(FP8X4),
+                        rhs=xg_w[:, own].bitcast(FP8X4),
                         rhs_scale=xg_s[:, cols],
                         start=True,
                         stop=False,
@@ -205,63 +232,62 @@ def tile_moe_elr_s_relu_kernel(
                         start=False,
                         stop=True,
                     )
-                if (e, u) == (E - 1, 1):
+                if e < E - 1:
+                    nc.scalar.copy(out=y[:, :, place], in_=bank[:])
+                else:
                     y_bf = ring.tile([P, HALF * PACK], BF16, name="y_bf", align_bytes=64)
-                    nc.vector.tensor_copy(
-                        out=y_bf[:].rearrange("p (s t) -> p s t", t=PACK), in_=bank[:].rearrange("p t s -> p s t")
-                    )
-                    st[e, "y_bf", HALF] = y_bf
-                nc.scalar.copy(out=y[:, :, own], in_=bank[:])
-                if e == E - 1:
-                    nc.sync.dma_start(out=rows_out[:, :, e * C + u * HALF : e * C + (u + 1) * HALF], in_=y[:, :, own])
-            if e < E - 1:
-                nc.sync.dma_start(out=rows_out[:, :, e * C : (e + 1) * C], in_=y[:])
-            st[e, "y"] = y
+                    nc.scalar.copy(out=y_bf[:].rearrange("p (s t) -> p s t", t=PACK), in_=bank[:].rearrange("p t s -> p s t"))
+                    st[e * C + u * HALF, "y_bf"] = y_bf
+                    if u == 0:
+                        nc.vector.tensor_copy(out=y[:, :, place], in_=bank[:])
+                    else:
+                        nc.scalar.copy(out=y[:, :, place], in_=bank[:])
+                    nc.sync.dma_start(out=rows_out[:, :, e * C + u * HALF : e * C + (u + 1) * HALF], in_=y[:, :, place])
+            if e == e1 - 1 and e < E - 1:
+                nc.sync.dma_start(out=rows_out[:, :, e0 * C : e1 * C], in_=y[:])
 
-        def round_y(e, c0, c1):
-            y_bf = ring.tile([P, (c1 - c0) * PACK], BF16, name="y_bf", align_bytes=64)
+        def round_y(e0, e1):
+            y_bf = ring.tile([P, (e1 - e0) * C * PACK], BF16, name="y_bf", align_bytes=64)
             nc.vector.tensor_copy(
                 out=y_bf[:].rearrange("p (c i t) -> p c t i", i=4, t=PACK),
-                in_=st[e, "y"][:, :, c0:c1].rearrange("p t (c i) -> p c t i", i=4),
+                in_=st[e0, "y"][:].rearrange("p t (c i) -> p c t i", i=4),
             )
-            st[e, "y_bf", c0] = y_bf
+            st[e0 * C, "y_bf"] = y_bf
 
-        def quant_y(e, c0, c1):
-            nc.vector.quantize_mx(
-                out=y_words[:, e * C + c0 : e * C + c1].bitcast(FP8X4),
-                scales=y_scales[:, e * C + c0 : e * C + c1],
-                in_=st[e, "y_bf", c0][:],
-            )
+        def quant_y(s0, s1):
+            nc.vector.quantize_mx(out=y_words[:, s0:s1].bitcast(FP8X4), scales=y_scales[:, s0:s1], in_=st[s0, "y_bf"][:])
 
         def store_words(s0, s1):
             nc.sync.dma_start(out=words_out[:, 4 * s0 : 4 * s1].bitcast(I32), in_=y_words[:, s0:s1].bitcast(I32))
 
         for pair in range(E // 2):
             gather_scales(pair)
-        gather(0)
+        gather(0, 1)
         round_wb(0)
-        gather(1)
-        deal(0)
-        hidden(0)
-        for s in range(E):
-            quant_wb(s)
-            quant_h(s)
+        gather(1, 3)
+        group_end = {e1 - 1: e0 for e0, e1 in OUT_GROUPS[:-1]}
+        for s in range(E + 1):
+            if s < E:
+                deal(s)
+                hidden(s)
+                quant_wb(s)
+            if s - 2 in group_end:
+                quant_y(group_end[s - 2] * C, (s - 1) * C)
+                if s < E:
+                    store_words(group_end[s - 2] * C, (s - 1) * C)
+            if s >= 1:
+                result(s - 1)
+            if s < E:
+                quant_h(s)
             if s + 1 < E:
-                deal(s + 1)
-                hidden(s + 1)
                 round_wb(s + 1)
-            if s + 2 < E:
-                gather(s + 2)
-            result(s)
-            if s + 1 < E:
-                round_y(s, 0, C)
-                quant_y(s, 0, C)
-            if s in (1, 3):
-                store_words((s - 1) * C, (s + 1) * C)
-        round_y(E - 1, 0, HALF)
-        quant_y(E - 1, 0, HALF)
+            if s >= 1 and s + 2 in in_group:
+                gather(s + 2, in_group[s + 2])
+            if s - 1 in group_end:
+                round_y(group_end[s - 1], s)
+        quant_y((E - 1) * C, E * C - HALF)
         store_words((E - 2) * C, E * C - HALF)
-        quant_y(E - 1, HALF, C)
+        quant_y(E * C - HALF, E * C)
         store_words(E * C - HALF, E * C)
         by_row = out_2[0].rearrange("(q r) s -> r q s", r=4)
         for r in range(4):

@@ -19,8 +19,8 @@ P = 128
 PACK = 4
 HALF = 128
 WA_ROW = 4
-VECTOR_FROM = 2
-SPLIT_LOADS = 2
+VECTOR_FROM = 3
+SPLIT_LOADS = 1
 IN_GROUPS = [(0, 1), (1, 3), (3, 5), (5, 6)]
 OUT_GROUPS = [(0, 2), (2, 4), (4, 5), (5, 6)]
 
@@ -66,6 +66,9 @@ def tile_moe_elr_s_relu_kernel(
         def load_wb_half(e, u):
             nc.sync.dma_start(out=wb_half[e, u], in_=wb_rows(e)[:, :, u * (N // 2) : (u + 1) * (N // 2)])
 
+        def load_wb(e):
+            nc.sync.dma_start(out=wb_half[e][:], in_=wb_rows(e))
+
         def load_scale_rows(row, scales):
             by_row = scales[:, 0].rearrange("e (q r) n -> r q e n", r=4)
             for r in range(4):
@@ -79,16 +82,16 @@ def tile_moe_elr_s_relu_kernel(
         nc.sync.dma_start(out=xw[:].bitcast(I32), in_=x_words[0].rearrange("p t d -> p (t d)").bitcast(I32))
         load_wb_half(0, 1)
         load_scale_rows(WA_ROW, wa_scales)
-        load_wb_half(1, 0)
+        load_wb(1)
         load_wa(0, 1)
         load_scale_rows(0, w_scales)
-        load_wb_half(1, 1)
+        load_wb(2)
         load_w(0, 1)
         for e0, e1 in IN_GROUPS[1:]:
             load_wa(e0, e1)
             load_w(e0, e1)
-            for e in range(e0 + 1, min(e1 + 1, E)):
-                nc.sync.dma_start(out=wb_half[e][:], in_=wb_rows(e))
+            for e in range(max(e0 + 1, 3), min(e1 + 1, E)):
+                load_wb(e)
 
         tok = {}
         st = {}
@@ -99,7 +102,7 @@ def tile_moe_elr_s_relu_kernel(
             st[pair, "xg_scales"] = scales
 
         def gather(e0, e1):
-            words = ring.tile([P, (e1 - e0) * C], U32, name="xg_words", align_bytes=64, bufs=2)
+            words = keep.tile([P, (e1 - e0) * C], U32, name="xg_words%d" % e0, align_bytes=64)
             nc.vector.tensor_copy(words[:], xw[:].indirect(offsets[:, e0 * C // 16 : e1 * C // 16]))
             for e in range(e0, e1):
                 tok[e] = (words[:, (e - e0) * C : (e - e0 + 1) * C], st[e // 2, "xg_scales"], (e % 2) * C)
@@ -145,7 +148,7 @@ def tile_moe_elr_s_relu_kernel(
             for u in range(2):
                 dst = wb_bf[:, :, u * 64 : (u + 1) * 64, :].rearrange("p t m j -> p m j t")
                 src = wb_half[e, u].rearrange("p j (m t) -> p m j t", t=PACK)
-                if (u == 1 and e >= VECTOR_FROM) or e == E - 1:
+                if u == 1 and e >= VECTOR_FROM:
                     nc.vector.tensor_copy(out=dst, in_=src)
                 else:
                     nc.scalar.copy(out=dst, in_=src)
@@ -273,8 +276,7 @@ def tile_moe_elr_s_relu_kernel(
                 quant_wb(s)
             if s - 2 in group_end:
                 quant_y(group_end[s - 2] * C, (s - 1) * C)
-                if s < E:
-                    store_words(group_end[s - 2] * C, (s - 1) * C)
+                store_words(group_end[s - 2] * C, (s - 1) * C)
             if s >= 1:
                 result(s - 1)
             if s < E:
@@ -286,9 +288,8 @@ def tile_moe_elr_s_relu_kernel(
             if s - 1 in group_end:
                 round_y(group_end[s - 1], s)
         quant_y((E - 1) * C, E * C - HALF)
-        store_words((E - 2) * C, E * C - HALF)
         quant_y(E * C - HALF, E * C)
-        store_words(E * C - HALF, E * C)
+        store_words((E - 1) * C, E * C)
         by_row = out_2[0].rearrange("(q r) s -> r q s", r=4)
         for r in range(4):
             nc.scalar.dma_start(out=by_row[r].bitcast(I32), in_=y_scales[r:P:32, :].bitcast(I32))

@@ -19,9 +19,11 @@ P = 128
 PACK = 4
 HALF = 128
 WA_ROW = 4
+SPLIT_LOADS = 2
 VECTOR_FROM = 3
-SPLIT_LOADS = 1
-IN_GROUPS = [(0, 1), (1, 3), (3, 5), (5, 6)]
+SC_GROUPS = [(0, 2), (2, 6)]
+WA_GROUPS = [(0, 2), (2, 6)]
+W_GROUPS = [(0, 2), (2, 6)]
 OUT_GROUPS = [(0, 2), (2, 4), (4, 5), (5, 6)]
 
 
@@ -32,23 +34,21 @@ def tile_moe_elr_s_relu_kernel(
     with ExitStack() as ctx:
         keep = ctx.enter_context(tc.tile_pool(name="keep", bufs=1))
         ring = ctx.enter_context(tc.tile_pool(name="ring", bufs=3))
-        psum = ctx.enter_context(tc.psum_pool(name="psum", bufs=4))
+        psum = ctx.enter_context(tc.psum_pool(name="psum", bufs=1))
 
         offsets = keep.tile([P, E * C // 16], U16, name="offsets")
         xw = keep.tile([P, T], U32, name="xw", align_bytes=64)
         xs = keep.tile([P, T], U8, name="xs", align_bytes=64)
         sc_raw = keep.tile([P, E, N], U8, name="sc_raw", align_bytes=64)
-        wb_half = {}
+        wb_raw = {}
         for e in range(E):
             if e < SPLIT_LOADS:
                 for u in range(2):
-                    wb_half[e, u] = keep.tile([P, PACK, N // 2], F32, name="wb_raw%d_%d" % (e, u), align_bytes=64)[:]
+                    wb_raw[e, u] = keep.tile([P, PACK, N // 2], F32, name="wb_raw%d_%d" % (e, u), align_bytes=64)
             else:
-                wb_half[e] = keep.tile([P, PACK, N], F32, name="wb_raw%d" % e, align_bytes=64)
-                for u in range(2):
-                    wb_half[e, u] = wb_half[e][:, :, u * (N // 2) : (u + 1) * (N // 2)]
-        wa_raw = {e0: keep.tile([P, e1 - e0, H], I32, name="wa_raw%d" % e0, align_bytes=64) for e0, e1 in IN_GROUPS}
-        w_raw = {e0: keep.tile([P, e1 - e0, 2 * N], U8, name="w_raw%d" % e0, align_bytes=64) for e0, e1 in IN_GROUPS}
+                wb_raw[e] = keep.tile([P, PACK, N], F32, name="wb_raw%d" % e, align_bytes=64)
+        wa_raw = {e0: keep.tile([P, e1 - e0, H], I32, name="wa_raw%d" % e0, align_bytes=64) for e0, e1 in WA_GROUPS}
+        w_raw = {e0: keep.tile([P, e1 - e0, 2 * N], U8, name="w_raw%d" % e0, align_bytes=64) for e0, e1 in W_GROUPS}
         y_words = keep.tile([P, E * C], U32, name="y_words", align_bytes=64)
         y_scales = keep.tile([P, E * C], U8, name="y_scales", align_bytes=64)
 
@@ -64,15 +64,14 @@ def tile_moe_elr_s_relu_kernel(
             nc.sync.dma_start(out=w_raw[e0][:].bitcast(I32), in_=w_words[e0:e1, 0].rearrange("e p b -> p e b").bitcast(I32))
 
         def load_wb_half(e, u):
-            nc.sync.dma_start(out=wb_half[e, u], in_=wb_rows(e)[:, :, u * (N // 2) : (u + 1) * (N // 2)])
+            nc.sync.dma_start(out=wb_raw[e, u][:], in_=wb_rows(e)[:, :, u * (N // 2) : (u + 1) * (N // 2)])
 
         def load_wb(e):
-            nc.sync.dma_start(out=wb_half[e][:], in_=wb_rows(e))
+            nc.sync.dma_start(out=wb_raw[e][:], in_=wb_rows(e))
 
-        def load_scale_rows(row, scales):
+        def load_scale_row(row, scales, r):
             by_row = scales[:, 0].rearrange("e (q r) n -> r q e n", r=4)
-            for r in range(4):
-                nc.sync.dma_start(out=sc_raw[row + r : P : 32, :, :].bitcast(I32), in_=by_row[r].bitcast(I32))
+            nc.sync.dma_start(out=sc_raw[row + r : P : 32, :, :].bitcast(I32), in_=by_row[r].bitcast(I32))
 
         nc.sync.dma_start(offsets[:], offs)
         for q in range(4):
@@ -81,34 +80,34 @@ def tile_moe_elr_s_relu_kernel(
         load_wb_half(0, 0)
         nc.sync.dma_start(out=xw[:].bitcast(I32), in_=x_words[0].rearrange("p t d -> p (t d)").bitcast(I32))
         load_wb_half(0, 1)
-        load_scale_rows(WA_ROW, wa_scales)
-        load_wb(1)
-        load_wa(0, 1)
-        load_scale_rows(0, w_scales)
+        for r in range(4):
+            load_scale_row(WA_ROW, wa_scales, r)
+        load_wb_half(1, 0)
+        load_wa(*WA_GROUPS[0])
+        for r in range(4):
+            load_scale_row(0, w_scales, r)
+        load_wb_half(1, 1)
+        load_w(*W_GROUPS[0])
         load_wb(2)
-        load_w(0, 1)
-        for e0, e1 in IN_GROUPS[1:]:
-            load_wa(e0, e1)
-            load_w(e0, e1)
-            for e in range(max(e0 + 1, 3), min(e1 + 1, E)):
-                load_wb(e)
+        load_wa(*WA_GROUPS[1])
+        load_w(*W_GROUPS[1])
+        for e in range(3, E):
+            load_wb(e)
 
-        tok = {}
         st = {}
 
+        def gather_words(pair):
+            words = ring.tile([P, 2 * C], U32, name="xg_words", align_bytes=64, bufs=2)
+            nc.vector.tensor_copy(words[:], xw[:].indirect(offsets[:, pair * C // 8 : (pair + 1) * C // 8]))
+            st[pair, "xg_words"] = words
+
         def gather_scales(pair):
-            scales = keep.tile([P, 2 * C], U8, name="xg_scales%d" % pair, align_bytes=64)
+            scales = ring.tile([P, 2 * C], U8, name="xg_scales", align_bytes=64, bufs=2)
             nc.vector.tensor_copy(scales[:], xs[:].indirect(offsets[:, pair * C // 8 : (pair + 1) * C // 8]))
             st[pair, "xg_scales"] = scales
 
-        def gather(e0, e1):
-            words = keep.tile([P, (e1 - e0) * C], U32, name="xg_words%d" % e0, align_bytes=64)
-            nc.vector.tensor_copy(words[:], xw[:].indirect(offsets[:, e0 * C // 16 : e1 * C // 16]))
-            for e in range(e0, e1):
-                tok[e] = (words[:, (e - e0) * C : (e - e0 + 1) * C], st[e // 2, "xg_scales"], (e % 2) * C)
-
         def deal_wa(e0, e1):
-            wa_p = ring.tile([P, e1 - e0, H], I32, name="wa_p", align_bytes=64, bufs=2)
+            wa_p = keep.tile([P, e1 - e0, H], I32, name="wa_p%d" % e0, align_bytes=64)
             nc.vector.tensor_copy(
                 out=wa_p[:].rearrange("p e (t m) -> p e m t", t=PACK),
                 in_=wa_raw[e0][:].rearrange("p e (m t) -> p e m t", t=PACK),
@@ -117,7 +116,7 @@ def tile_moe_elr_s_relu_kernel(
                 st[e, "wa"] = wa_p[:, e - e0, :]
 
         def deal_w(e0, e1):
-            w_p = ring.tile([P, e1 - e0, 2 * N], U8, name="w_p", align_bytes=64, bufs=2)
+            w_p = keep.tile([P, e1 - e0, 2 * N], U8, name="w_p%d" % e0, align_bytes=64)
             nc.vector.tensor_copy(
                 out=w_p[:].bitcast(U16).rearrange("p e (t m) -> p e t m", t=PACK),
                 in_=w_raw[e0][:].bitcast(U16).rearrange("p e (m t) -> p e t m", t=PACK),
@@ -125,33 +124,31 @@ def tile_moe_elr_s_relu_kernel(
             for e in range(e0, e1):
                 st[e, "w"] = w_p[:, e - e0, :]
 
-        def deal_scales(e):
-            sc_p = ring.tile([P, 2, N], U8, name="sc_p", align_bytes=64, bufs=2)
+        def deal_scales(e0, e1):
+            sc_p = keep.tile([P, e1 - e0, N], U8, name="sc_p%d" % e0, align_bytes=64)
             nc.vector.tensor_copy(
                 out=sc_p[:].rearrange("p e (t m) -> p e t m", t=PACK),
-                in_=sc_raw[:, e : e + 2, :].rearrange("p e (m t) -> p e t m", t=PACK),
+                in_=sc_raw[:, e0:e1, :].rearrange("p e (m t) -> p e t m", t=PACK),
             )
-            st[e, "sc"] = st[e + 1, "sc"] = sc_p
-
-        in_group = dict(IN_GROUPS)
-
-        def deal(e):
-            if e in in_group:
-                deal_wa(e, in_group[e])
-            if e % 2 == 0:
-                deal_scales(e)
-            if e in in_group:
-                deal_w(e, in_group[e])
+            for e in range(e0, e1):
+                st[e, "sc"] = sc_p[:, e - e0, :]
 
         def round_wb(e):
             wb_bf = ring.tile([P, PACK, P, PACK], BF16, name="wb_bf", align_bytes=64)
-            for u in range(2):
-                dst = wb_bf[:, :, u * 64 : (u + 1) * 64, :].rearrange("p t m j -> p m j t")
-                src = wb_half[e, u].rearrange("p j (m t) -> p m j t", t=PACK)
-                if u == 1 and e >= VECTOR_FROM:
-                    nc.vector.tensor_copy(out=dst, in_=src)
-                else:
-                    nc.scalar.copy(out=dst, in_=src)
+            if SPLIT_LOADS <= e < VECTOR_FROM:
+                nc.scalar.copy(
+                    out=wb_bf[:].rearrange("p t m j -> p m j t"),
+                    in_=wb_raw[e][:].rearrange("p j (m t) -> p m j t", t=PACK),
+                )
+            else:
+                for u in range(2):
+                    raw = wb_raw[e, u][:] if e < SPLIT_LOADS else wb_raw[e][:, :, u * (N // 2) : (u + 1) * (N // 2)]
+                    dst = wb_bf[:, :, u * 64 : (u + 1) * 64, :].rearrange("p t m j -> p m j t")
+                    src = raw.rearrange("p j (m t) -> p m j t", t=PACK)
+                    if e >= VECTOR_FROM and u == 1:
+                        nc.vector.tensor_copy(out=dst, in_=src)
+                    else:
+                        nc.scalar.copy(out=dst, in_=src)
             st[e, "wb_bf"] = wb_bf
 
         def quant_wb(e):
@@ -163,18 +160,18 @@ def tile_moe_elr_s_relu_kernel(
             st[e, "wbq"] = (words, scales)
 
         def hidden(e):
-            xg_w, xg_s, c0 = tok[e]
+            xg_w, xg_s = st[e // 2, "xg_words"], st[e // 2, "xg_scales"]
             h_bf = ring.tile([P, C, PACK], BF16, name="h_bf", align_bytes=64)
             for u in range(C // HALF):
-                cols = slice(c0 + u * HALF, c0 + (u + 1) * HALF)
-                bank = psum.tile([P, PACK, HALF], F32, name="h_bank")
+                cols = slice((e % 2) * C + u * HALF, (e % 2) * C + (u + 1) * HALF)
+                bank = psum.tile([P, PACK, HALF], F32, name="h_bank", bufs=4)
                 for t in range(PACK):
                     m = slice(t * P, (t + 1) * P)
                     nc.tensor.matmul_mx(
                         out=bank[:, t, :],
                         lhsT=st[e, "wa"][:, m].bitcast(FP8X4),
-                        lhsT_scale=st[e, "sc"][WA_ROW:P, e % 2, m],
-                        rhs=xg_w[:, u * HALF : (u + 1) * HALF].bitcast(FP8X4),
+                        lhsT_scale=st[e, "sc"][WA_ROW:P, m],
+                        rhs=xg_w[:, cols].bitcast(FP8X4),
                         rhs_scale=xg_s[:, cols],
                         start=True,
                         stop=True,
@@ -187,14 +184,9 @@ def tile_moe_elr_s_relu_kernel(
         def quant_h(e):
             words = ring.tile([P, C], U32, name="h_words", align_bytes=64)
             scales = ring.tile([P, C], U8, name="h_scales", align_bytes=64)
-            width = HALF if e == E - 1 else C
-            for c0 in range(0, C, width):
-                cols = slice(c0, c0 + width)
-                nc.vector.quantize_mx(
-                    out=words[:, cols].bitcast(FP8X4),
-                    scales=scales[:, cols],
-                    in_=st[e, "h_bf"][:, cols, :].rearrange("p s t -> p (s t)"),
-                )
+            nc.vector.quantize_mx(
+                out=words[:].bitcast(FP8X4), scales=scales[:], in_=st[e, "h_bf"][:].rearrange("p s t -> p (s t)")
+            )
             st[e, "hq"] = (words, scales)
 
         rows_out = out_0.rearrange("(p t) s -> p t s", t=PACK)
@@ -203,25 +195,26 @@ def tile_moe_elr_s_relu_kernel(
         out_group = {e: (e0, e1) for e0, e1 in OUT_GROUPS for e in range(e0, e1)}
 
         def result(e):
-            xg_w, xg_s, c0 = tok[e]
+            xg_w, xg_s = st[e // 2, "xg_words"], st[e // 2, "xg_scales"]
             wb_w, wb_s = st[e, "wbq"]
             h_w, h_s = st[e, "hq"]
             e0, e1 = out_group[e]
             if e == e0:
                 st[e0, "y"] = keep.tile([P, PACK, (e1 - e0) * C], F32, name="y%d" % e0, align_bytes=64)
-            y = st[e0, "y"]
+                st[e0, "y_bf"] = keep.tile([P, (e1 - e0) * C, PACK], BF16, name="y_bf%d" % e0, align_bytes=64)
+            y, y_bf = st[e0, "y"], st[e0, "y_bf"]
             for u in range(C // HALF):
-                cols = slice(c0 + u * HALF, c0 + (u + 1) * HALF)
+                cols = slice((e % 2) * C + u * HALF, (e % 2) * C + (u + 1) * HALF)
                 own = slice(u * HALF, (u + 1) * HALF)
                 place = slice((e - e0) * C + u * HALF, (e - e0) * C + (u + 1) * HALF)
-                bank = psum.tile([P, PACK, HALF], F32, name="y_bank")
+                bank = psum.tile([P, PACK, HALF], F32, name="y_bank", bufs=4)
                 for t in range(PACK):
                     m = slice(t * P, (t + 1) * P)
                     nc.tensor.matmul_mx(
                         out=bank[:, t, :],
                         lhsT=st[e, "w"][:, 2 * t * P : 2 * (t + 1) * P].bitcast(FP4X4),
-                        lhsT_scale=st[e, "sc"][:, e % 2, m],
-                        rhs=xg_w[:, own].bitcast(FP8X4),
+                        lhsT_scale=st[e, "sc"][:, m],
+                        rhs=xg_w[:, cols].bitcast(FP8X4),
                         rhs_scale=xg_s[:, cols],
                         start=True,
                         stop=False,
@@ -238,9 +231,7 @@ def tile_moe_elr_s_relu_kernel(
                 if e < E - 1:
                     nc.scalar.copy(out=y[:, :, place], in_=bank[:])
                 else:
-                    y_bf = ring.tile([P, HALF * PACK], BF16, name="y_bf", align_bytes=64)
-                    nc.scalar.copy(out=y_bf[:].rearrange("p (s t) -> p s t", t=PACK), in_=bank[:].rearrange("p t s -> p s t"))
-                    st[e * C + u * HALF, "y_bf"] = y_bf
+                    nc.scalar.copy(out=y_bf[:, place, :], in_=bank[:].rearrange("p t s -> p s t"))
                     if u == 0:
                         nc.vector.tensor_copy(out=y[:, :, place], in_=bank[:])
                     else:
@@ -249,47 +240,58 @@ def tile_moe_elr_s_relu_kernel(
             if e == e1 - 1 and e < E - 1:
                 nc.sync.dma_start(out=rows_out[:, :, e0 * C : e1 * C], in_=y[:])
 
-        def round_y(e0, e1):
-            y_bf = ring.tile([P, (e1 - e0) * C * PACK], BF16, name="y_bf", align_bytes=64)
+        def round_y(e0):
             nc.vector.tensor_copy(
-                out=y_bf[:].rearrange("p (c i t) -> p c t i", i=4, t=PACK),
+                out=st[e0, "y_bf"][:].rearrange("p (c i) t -> p c t i", i=4),
                 in_=st[e0, "y"][:].rearrange("p t (c i) -> p c t i", i=4),
             )
-            st[e0 * C, "y_bf"] = y_bf
 
-        def quant_y(s0, s1):
-            nc.vector.quantize_mx(out=y_words[:, s0:s1].bitcast(FP8X4), scales=y_scales[:, s0:s1], in_=st[s0, "y_bf"][:])
+        def quant_y(e0, e1):
+            width = HALF if e0 == E - 1 else (e1 - e0) * C
+            for c0 in range(0, (e1 - e0) * C, width):
+                cols = slice(e0 * C + c0, e0 * C + c0 + width)
+                nc.vector.quantize_mx(
+                    out=y_words[:, cols].bitcast(FP8X4),
+                    scales=y_scales[:, cols],
+                    in_=st[e0, "y_bf"][:, c0 : c0 + width, :].rearrange("p s t -> p (s t)"),
+                )
+            nc.sync.dma_start(
+                out=words_out[:, 4 * e0 * C : 4 * e1 * C].bitcast(I32), in_=y_words[:, e0 * C : e1 * C].bitcast(I32)
+            )
 
-        def store_words(s0, s1):
-            nc.sync.dma_start(out=words_out[:, 4 * s0 : 4 * s1].bitcast(I32), in_=y_words[:, s0:s1].bitcast(I32))
-
-        for pair in range(E // 2):
-            gather_scales(pair)
-        gather(0, 1)
-        round_wb(0)
-        gather(1, 3)
+        wa_group, w_group, sc_group = dict(WA_GROUPS), dict(W_GROUPS), dict(SC_GROUPS)
         group_end = {e1 - 1: e0 for e0, e1 in OUT_GROUPS[:-1]}
+
+        def gather(pair):
+            gather_scales(pair)
+            gather_words(pair)
+
+        gather(0)
+        round_wb(0)
+        gather(1)
         for s in range(E + 1):
             if s < E:
-                deal(s)
+                if s in wa_group:
+                    deal_wa(s, wa_group[s])
+                if s in sc_group:
+                    deal_scales(s, sc_group[s])
+                if s in w_group:
+                    deal_w(s, w_group[s])
                 hidden(s)
                 quant_wb(s)
             if s - 2 in group_end:
-                quant_y(group_end[s - 2] * C, (s - 1) * C)
-                store_words(group_end[s - 2] * C, (s - 1) * C)
+                quant_y(group_end[s - 2], s - 1)
             if s >= 1:
                 result(s - 1)
             if s < E:
                 quant_h(s)
             if s + 1 < E:
                 round_wb(s + 1)
-            if s >= 1 and s + 2 in in_group:
-                gather(s + 2, in_group[s + 2])
+            if s == 2:
+                gather(2)
             if s - 1 in group_end:
-                round_y(group_end[s - 1], s)
-        quant_y((E - 1) * C, E * C - HALF)
-        quant_y(E * C - HALF, E * C)
-        store_words((E - 1) * C, E * C)
+                round_y(group_end[s - 1])
+        quant_y(E - 1, E)
         by_row = out_2[0].rearrange("(q r) s -> r q s", r=4)
         for r in range(4):
             nc.scalar.dma_start(out=by_row[r].bitcast(I32), in_=y_scales[r:P:32, :].bitcast(I32))

@@ -19,10 +19,12 @@ P = 128
 PACK = 4
 HALF = 128
 WA_ROW = 4
-SPLIT_LOADS = 2
-VECTOR_FROM = 3
+SPLIT_LOADS = 1
+SCALAR_HALVES = 9
+WB_AHEAD = 3
+H_AHEAD = 2
 SC_GROUPS = [(0, 2), (2, 6)]
-WA_GROUPS = [(0, 2), (2, 6)]
+WA_GROUPS = [(0, 1), (1, 3), (3, 5), (5, 6)]
 W_GROUPS = [(0, 2), (2, 6)]
 OUT_GROUPS = [(0, 2), (2, 4), (4, 5), (5, 6)]
 
@@ -47,7 +49,7 @@ def tile_moe_elr_s_relu_kernel(
                     wb_raw[e, u] = keep.tile([P, PACK, N // 2], F32, name="wb_raw%d_%d" % (e, u), align_bytes=64)
             else:
                 wb_raw[e] = keep.tile([P, PACK, N], F32, name="wb_raw%d" % e, align_bytes=64)
-        wa_raw = {e0: keep.tile([P, e1 - e0, H], I32, name="wa_raw%d" % e0, align_bytes=64) for e0, e1 in WA_GROUPS}
+        wa_raw = {e0: keep.tile([P, e1 - e0, H], I32, name="wa_raw%d" % e0, tag="wa_raw%d" % e0, align_bytes=64) for e0, e1 in WA_GROUPS}
         w_raw = {e0: keep.tile([P, e1 - e0, 2 * N], U8, name="w_raw%d" % e0, align_bytes=64) for e0, e1 in W_GROUPS}
         y_words = keep.tile([P, E * C], U32, name="y_words", align_bytes=64)
         y_scales = keep.tile([P, E * C], U8, name="y_scales", align_bytes=64)
@@ -82,27 +84,29 @@ def tile_moe_elr_s_relu_kernel(
         load_wb_half(0, 1)
         for r in range(4):
             load_scale_row(WA_ROW, wa_scales, r)
-        load_wb_half(1, 0)
-        load_wa(*WA_GROUPS[0])
+        load_wb(1)
         for r in range(4):
             load_scale_row(0, w_scales, r)
-        load_wb_half(1, 1)
-        load_w(*W_GROUPS[0])
         load_wb(2)
+        load_wa(*WA_GROUPS[0])
         load_wa(*WA_GROUPS[1])
+        load_w(*W_GROUPS[0])
+        load_wb(3)
         load_w(*W_GROUPS[1])
-        for e in range(3, E):
-            load_wb(e)
+        load_wa(*WA_GROUPS[2])
+        load_wb(4)
+        load_wa(*WA_GROUPS[3])
+        load_wb(5)
 
         st = {}
 
         def gather_words(pair):
-            words = ring.tile([P, 2 * C], U32, name="xg_words", align_bytes=64, bufs=2)
+            words = ring.tile([P, 2 * C], U32, name="xg_words", align_bytes=64)
             nc.vector.tensor_copy(words[:], xw[:].indirect(offsets[:, pair * C // 8 : (pair + 1) * C // 8]))
             st[pair, "xg_words"] = words
 
         def gather_scales(pair):
-            scales = ring.tile([P, 2 * C], U8, name="xg_scales", align_bytes=64, bufs=2)
+            scales = ring.tile([P, 2 * C], U8, name="xg_scales", align_bytes=64)
             nc.vector.tensor_copy(scales[:], xs[:].indirect(offsets[:, pair * C // 8 : (pair + 1) * C // 8]))
             st[pair, "xg_scales"] = scales
 
@@ -125,7 +129,7 @@ def tile_moe_elr_s_relu_kernel(
                 st[e, "w"] = w_p[:, e - e0, :]
 
         def deal_scales(e0, e1):
-            sc_p = keep.tile([P, e1 - e0, N], U8, name="sc_p%d" % e0, align_bytes=64)
+            sc_p = keep.tile([P, e1 - e0, N], U8, name="sc_p%d" % e0, tag="wa_raw0" if e0 else "sc_p0", align_bytes=64)
             nc.vector.tensor_copy(
                 out=sc_p[:].rearrange("p e (t m) -> p e t m", t=PACK),
                 in_=sc_raw[:, e0:e1, :].rearrange("p e (m t) -> p e t m", t=PACK),
@@ -135,25 +139,26 @@ def tile_moe_elr_s_relu_kernel(
 
         def round_wb(e):
             wb_bf = ring.tile([P, PACK, P, PACK], BF16, name="wb_bf", align_bytes=64)
-            if SPLIT_LOADS <= e < VECTOR_FROM:
-                nc.scalar.copy(
-                    out=wb_bf[:].rearrange("p t m j -> p m j t"),
-                    in_=wb_raw[e][:].rearrange("p j (m t) -> p m j t", t=PACK),
-                )
+            on_scalar = [2 * e + u < SCALAR_HALVES for u in range(2)]
+            if e >= SPLIT_LOADS and on_scalar[0] == on_scalar[1]:
+                parts = [(wb_bf[:], wb_raw[e][:], on_scalar[0])]
             else:
+                parts = []
                 for u in range(2):
                     raw = wb_raw[e, u][:] if e < SPLIT_LOADS else wb_raw[e][:, :, u * (N // 2) : (u + 1) * (N // 2)]
-                    dst = wb_bf[:, :, u * 64 : (u + 1) * 64, :].rearrange("p t m j -> p m j t")
-                    src = raw.rearrange("p j (m t) -> p m j t", t=PACK)
-                    if e >= VECTOR_FROM and u == 1:
-                        nc.vector.tensor_copy(out=dst, in_=src)
-                    else:
-                        nc.scalar.copy(out=dst, in_=src)
+                    parts.append((wb_bf[:, :, u * 64 : (u + 1) * 64, :], raw, on_scalar[u]))
+            for dst, raw, scalar in parts:
+                dst = dst.rearrange("p t m j -> p m j t")
+                src = raw.rearrange("p j (m t) -> p m j t", t=PACK)
+                if scalar:
+                    nc.scalar.copy(out=dst, in_=src)
+                else:
+                    nc.vector.tensor_copy(out=dst, in_=src)
             st[e, "wb_bf"] = wb_bf
 
         def quant_wb(e):
-            words = ring.tile([P, N], U32, name="wb_words", align_bytes=64)
-            scales = ring.tile([P, N], U8, name="wb_scales", align_bytes=64)
+            words = ring.tile([P, N], U32, name="wb_words", align_bytes=64, bufs=E)
+            scales = ring.tile([P, N], U8, name="wb_scales", align_bytes=64, bufs=E)
             nc.vector.quantize_mx(
                 out=words[:].bitcast(FP8X4), scales=scales[:], in_=st[e, "wb_bf"][:].rearrange("p t m j -> p (t m j)")
             )
@@ -161,7 +166,7 @@ def tile_moe_elr_s_relu_kernel(
 
         def hidden(e):
             xg_w, xg_s = st[e // 2, "xg_words"], st[e // 2, "xg_scales"]
-            h_bf = ring.tile([P, C, PACK], BF16, name="h_bf", align_bytes=64)
+            h_bf = ring.tile([P, C, PACK], BF16, name="h_bf", align_bytes=64, bufs=E)
             for u in range(C // HALF):
                 cols = slice((e % 2) * C + u * HALF, (e % 2) * C + (u + 1) * HALF)
                 bank = psum.tile([P, PACK, HALF], F32, name="h_bank", bufs=4)
@@ -182,8 +187,8 @@ def tile_moe_elr_s_relu_kernel(
             st[e, "h_bf"] = h_bf
 
         def quant_h(e):
-            words = ring.tile([P, C], U32, name="h_words", align_bytes=64)
-            scales = ring.tile([P, C], U8, name="h_scales", align_bytes=64)
+            words = ring.tile([P, C], U32, name="h_words", align_bytes=64, bufs=E)
+            scales = ring.tile([P, C], U8, name="h_scales", align_bytes=64, bufs=E)
             nc.vector.quantize_mx(
                 out=words[:].bitcast(FP8X4), scales=scales[:], in_=st[e, "h_bf"][:].rearrange("p s t -> p (s t)")
             )
@@ -237,8 +242,10 @@ def tile_moe_elr_s_relu_kernel(
                     else:
                         nc.scalar.copy(out=y[:, :, place], in_=bank[:])
                     nc.sync.dma_start(out=rows_out[:, :, e * C + u * HALF : e * C + (u + 1) * HALF], in_=y[:, :, place])
-            if e == e1 - 1 and e < E - 1:
+            if e == 1:
                 nc.sync.dma_start(out=rows_out[:, :, e0 * C : e1 * C], in_=y[:])
+            elif 1 < e < E - 1:
+                nc.sync.dma_start(out=rows_out[:, :, e * C : (e + 1) * C], in_=y[:, :, (e - e0) * C : (e - e0 + 1) * C])
 
         def round_y(e0):
             nc.vector.tensor_copy(
@@ -260,37 +267,43 @@ def tile_moe_elr_s_relu_kernel(
             )
 
         wa_group, w_group, sc_group = dict(WA_GROUPS), dict(W_GROUPS), dict(SC_GROUPS)
+
+        for pair in range(E // 2):
+            gather_scales(pair)
+        for pair in range(E // 2):
+            gather_words(pair)
         group_end = {e1 - 1: e0 for e0, e1 in OUT_GROUPS[:-1]}
 
-        def gather(pair):
-            gather_scales(pair)
-            gather_words(pair)
+        def first_layer(e):
+            if e in wa_group:
+                deal_wa(e, wa_group[e])
+            if e in sc_group:
+                deal_scales(e, sc_group[e])
+            hidden(e)
 
-        gather(0)
-        round_wb(0)
-        gather(1)
-        for s in range(E + 1):
-            if s < E:
-                if s in wa_group:
-                    deal_wa(s, wa_group[s])
-                if s in sc_group:
-                    deal_scales(s, sc_group[s])
-                if s in w_group:
-                    deal_w(s, w_group[s])
-                hidden(s)
-                quant_wb(s)
-            if s - 2 in group_end:
-                quant_y(group_end[s - 2], s - 1)
-            if s >= 1:
-                result(s - 1)
-            if s < E:
-                quant_h(s)
-            if s + 1 < E:
-                round_wb(s + 1)
-            if s == 2:
-                gather(2)
-            if s - 1 in group_end:
-                round_y(group_end[s - 1])
+        def operands(e):
+            if e in w_group:
+                deal_w(e, w_group[e])
+            quant_wb(e)
+            quant_h(e)
+
+        for e in range(WB_AHEAD):
+            round_wb(e)
+        for e in range(H_AHEAD):
+            first_layer(e)
+        operands(0)
+        for e in range(E):
+            if e + H_AHEAD < E:
+                first_layer(e + H_AHEAD)
+            result(e)
+            if e + 1 < E:
+                operands(e + 1)
+            if e + WB_AHEAD < E:
+                round_wb(e + WB_AHEAD)
+            if e - 1 in group_end:
+                quant_y(group_end[e - 1], e)
+            if e in group_end:
+                round_y(group_end[e])
         quant_y(E - 1, E)
         by_row = out_2[0].rearrange("(q r) s -> r q s", r=4)
         for r in range(4):

@@ -20,7 +20,7 @@ PACK = 4
 HALF = 128
 WA_ROW = 4
 SPLIT_LOADS = 1
-SCALAR_HALVES = 9
+VECTOR_HALVES = [(4, 1), (5, 0), (5, 1)]
 WB_AHEAD = 3
 H_AHEAD = 2
 SC_GROUPS = [(0, 2), (2, 6)]
@@ -139,7 +139,7 @@ def tile_moe_elr_s_relu_kernel(
 
         def round_wb(e):
             wb_bf = ring.tile([P, PACK, P, PACK], BF16, name="wb_bf", align_bytes=64)
-            on_scalar = [2 * e + u < SCALAR_HALVES for u in range(2)]
+            on_scalar = [(e, u) not in VECTOR_HALVES for u in range(2)]
             if e >= SPLIT_LOADS and on_scalar[0] == on_scalar[1]:
                 parts = [(wb_bf[:], wb_raw[e][:], on_scalar[0])]
             else:
@@ -208,15 +208,14 @@ def tile_moe_elr_s_relu_kernel(
                 st[e0, "y"] = keep.tile([P, PACK, (e1 - e0) * C], F32, name="y%d" % e0, align_bytes=64)
                 st[e0, "y_bf"] = keep.tile([P, (e1 - e0) * C, PACK], BF16, name="y_bf%d" % e0, align_bytes=64)
             y, y_bf = st[e0, "y"], st[e0, "y_bf"]
-            for u in range(C // HALF):
-                cols = slice((e % 2) * C + u * HALF, (e % 2) * C + (u + 1) * HALF)
-                own = slice(u * HALF, (u + 1) * HALF)
-                place = slice((e - e0) * C + u * HALF, (e - e0) * C + (u + 1) * HALF)
-                bank = psum.tile([P, PACK, HALF], F32, name="y_bank", bufs=4)
-                for t in range(PACK):
-                    m = slice(t * P, (t + 1) * P)
+            halves = range(C // HALF)
+            banks = [psum.tile([P, PACK, HALF], F32, name="y_bank", bufs=4) for u in halves]
+            for t in range(PACK):
+                m = slice(t * P, (t + 1) * P)
+                for u in halves:
+                    cols = slice((e % 2) * C + u * HALF, (e % 2) * C + (u + 1) * HALF)
                     nc.tensor.matmul_mx(
-                        out=bank[:, t, :],
+                        out=banks[u][:, t, :],
                         lhsT=st[e, "w"][:, 2 * t * P : 2 * (t + 1) * P].bitcast(FP4X4),
                         lhsT_scale=st[e, "sc"][:, m],
                         rhs=xg_w[:, cols].bitcast(FP8X4),
@@ -224,8 +223,10 @@ def tile_moe_elr_s_relu_kernel(
                         start=True,
                         stop=False,
                     )
+                for u in halves:
+                    own = slice(u * HALF, (u + 1) * HALF)
                     nc.tensor.matmul_mx(
-                        out=bank[:, t, :],
+                        out=banks[u][:, t, :],
                         lhsT=wb_w[:, m].bitcast(FP8X4),
                         lhsT_scale=wb_s[:, m],
                         rhs=h_w[:, own].bitcast(FP8X4),
@@ -233,18 +234,18 @@ def tile_moe_elr_s_relu_kernel(
                         start=False,
                         stop=True,
                     )
+            for u in halves:
+                place = slice((e - e0) * C + u * HALF, (e - e0) * C + (u + 1) * HALF)
                 if e < E - 1:
-                    nc.scalar.copy(out=y[:, :, place], in_=bank[:])
+                    nc.scalar.copy(out=y[:, :, place], in_=banks[u][:])
                 else:
-                    nc.scalar.copy(out=y_bf[:, place, :], in_=bank[:].rearrange("p t s -> p s t"))
+                    nc.scalar.copy(out=y_bf[:, place, :], in_=banks[u][:].rearrange("p t s -> p s t"))
                     if u == 0:
-                        nc.vector.tensor_copy(out=y[:, :, place], in_=bank[:])
+                        nc.vector.tensor_copy(out=y[:, :, place], in_=banks[u][:])
                     else:
-                        nc.scalar.copy(out=y[:, :, place], in_=bank[:])
+                        nc.scalar.copy(out=y[:, :, place], in_=banks[u][:])
                     nc.sync.dma_start(out=rows_out[:, :, e * C + u * HALF : e * C + (u + 1) * HALF], in_=y[:, :, place])
-            if e == 1:
-                nc.sync.dma_start(out=rows_out[:, :, e0 * C : e1 * C], in_=y[:])
-            elif 1 < e < E - 1:
+            if e < E - 1:
                 nc.sync.dma_start(out=rows_out[:, :, e * C : (e + 1) * C], in_=y[:, :, (e - e0) * C : (e - e0 + 1) * C])
 
         def round_y(e0):

@@ -54,6 +54,7 @@ def tile_moe_elr_s_relu_kernel(
         y_words = keep.tile([P, E * C], U32, name="y_words", align_bytes=64)
         y_scales = keep.tile([P, E * C], U8, name="y_scales", align_bytes=64)
 
+        nc.gpsimd.memset(xs[:].bitcast(I32), 0)
         nc.gpsimd.memset(sc_raw[:].rearrange("p e n -> p (e n)").bitcast(I32), 0)
 
         def wb_rows(e):
@@ -76,11 +77,11 @@ def tile_moe_elr_s_relu_kernel(
             nc.sync.dma_start(out=sc_raw[row + r : P : 32, :, :].bitcast(I32), in_=by_row[r].bitcast(I32))
 
         nc.sync.dma_start(offsets[:], offs)
-        for q in range(4):
-            rows = x_scales[0, 4 * q : 4 * q + 4, :].bitcast(I32)
-            nc.sync.dma_start(out=xs[32 * q : 32 * q + 32, :].bitcast(I32), in_=rows.unsqueeze(0).to_broadcast([8, 4, T // 4]))
-        load_wb_half(0, 0)
         nc.sync.dma_start(out=xw[:].bitcast(I32), in_=x_words[0].rearrange("p t d -> p (t d)").bitcast(I32))
+        xs_rows = x_scales[0].rearrange("(q r) s -> r q s", r=4)
+        load_wb_half(0, 0)
+        for r in range(4):
+            nc.sync.dma_start(out=xs[r:P:32, :].bitcast(I32), in_=xs_rows[r].bitcast(I32))
         load_wb_half(0, 1)
         for r in range(4):
             load_scale_row(WA_ROW, wa_scales, r)
@@ -270,9 +271,9 @@ def tile_moe_elr_s_relu_kernel(
         wa_group, w_group, sc_group = dict(WA_GROUPS), dict(W_GROUPS), dict(SC_GROUPS)
 
         for pair in range(E // 2):
-            gather_scales(pair)
-        for pair in range(E // 2):
             gather_words(pair)
+        for pair in range(E // 2):
+            gather_scales(pair)
         group_end = {e1 - 1: e0 for e0, e1 in OUT_GROUPS[:-1]}
 
         def first_layer(e):

@@ -20,7 +20,7 @@ PACK = 4
 HALF = 128
 WA_ROW = 4
 SPLIT_LOADS = 1
-VECTOR_HALVES = [(4, 1), (5, 0), (5, 1)]
+VECTOR_HALVES = [(3, 1), (4, 1), (5, 0), (5, 1)]
 WB_AHEAD = 3
 H_AHEAD = 2
 SC_GROUPS = [(0, 2), (2, 6)]
@@ -264,9 +264,9 @@ def tile_moe_elr_s_relu_kernel(
                     scales=y_scales[:, cols],
                     in_=st[e0, "y_bf"][:, c0 : c0 + width, :].rearrange("p s t -> p (s t)"),
                 )
-            nc.sync.dma_start(
-                out=words_out[:, 4 * e0 * C : 4 * e1 * C].bitcast(I32), in_=y_words[:, e0 * C : e1 * C].bitcast(I32)
-            )
+            if e1 % 2 == 0:
+                cols = slice((e1 - 2) * C, e1 * C)
+                nc.sync.dma_start(out=words_out[:, 4 * cols.start : 4 * cols.stop].bitcast(I32), in_=y_words[:, cols].bitcast(I32))
 
         wa_group, w_group, sc_group = dict(WA_GROUPS), dict(W_GROUPS), dict(SC_GROUPS)
 

@@ -2,7 +2,7 @@ from contextlib import ExitStack
 
 import concourse.mybir as mybir
 
-K, T, E, C, H, N = 512, 768, 6, 256, 512, 512
+T, E, C, H, N = 768, 6, 256, 512, 512
 FLOPS = 3 * 2 * 512 * 512 * E * C
 
 F32 = mybir.dt.float32
@@ -18,15 +18,25 @@ RELU = mybir.ActivationFunctionType.Relu
 P = 128
 PACK = 4
 HALF = 128
+LIST_COLUMN = 16
+SCALE_ROWS = 4
 WA_ROW = 4
-SPLIT_LOADS = 1
-VECTOR_HALVES = [(3, 1), (4, 1), (5, 0), (5, 1)]
-WB_AHEAD = 3
+
+SCALAR_WB = 3
 H_AHEAD = 2
-SC_GROUPS = [(0, 2), (2, 6)]
+WB_AHEAD = 3
+
+PAIRS = [(e, e + 2) for e in range(0, E, 2)]
 WA_GROUPS = [(0, 1), (1, 3), (3, 5), (5, 6)]
 W_GROUPS = [(0, 2), (2, 6)]
-OUT_GROUPS = [(0, 2), (2, 4), (4, 5), (5, 6)]
+Y_GROUPS = [(0, 2), (2, 4), (4, 5), (5, 6)]
+VECTOR_ALONE = (2, 4)
+
+TAKES_OVER = {
+    "sc_dealt2": "wa_raw0",
+    "sc_dealt4": "wa_raw3",
+    "wb_words2": "w_raw0",
+}
 
 
 def tile_moe_elr_s_relu_kernel(
@@ -35,24 +45,22 @@ def tile_moe_elr_s_relu_kernel(
     nc = tc.nc
     with ExitStack() as ctx:
         keep = ctx.enter_context(tc.tile_pool(name="keep", bufs=1))
-        ring = ctx.enter_context(tc.tile_pool(name="ring", bufs=3))
-        psum = ctx.enter_context(tc.psum_pool(name="psum", bufs=1))
+        ring = ctx.enter_context(tc.tile_pool(name="ring", bufs=1))
+        psum = ctx.enter_context(tc.psum_pool(name="psum", bufs=4))
 
-        offsets = keep.tile([P, E * C // 16], U16, name="offsets")
-        xw = keep.tile([P, T], U32, name="xw", align_bytes=64)
-        xs = keep.tile([P, T], U8, name="xs", align_bytes=64)
-        sc_raw = keep.tile([P, E, N], U8, name="sc_raw", align_bytes=64)
-        wb_raw = {}
-        for e in range(E):
-            if e < SPLIT_LOADS:
-                for u in range(2):
-                    wb_raw[e, u] = keep.tile([P, PACK, N // 2], F32, name="wb_raw%d_%d" % (e, u), align_bytes=64)
-            else:
-                wb_raw[e] = keep.tile([P, PACK, N], F32, name="wb_raw%d" % e, align_bytes=64)
-        wa_raw = {e0: keep.tile([P, e1 - e0, H], I32, name="wa_raw%d" % e0, tag="wa_raw%d" % e0, align_bytes=64) for e0, e1 in WA_GROUPS}
-        w_raw = {e0: keep.tile([P, e1 - e0, 2 * N], U8, name="w_raw%d" % e0, align_bytes=64) for e0, e1 in W_GROUPS}
-        y_words = keep.tile([P, E * C], U32, name="y_words", align_bytes=64)
-        y_scales = keep.tile([P, E * C], U8, name="y_scales", align_bytes=64)
+        def kept(shape, dtype, name):
+            return keep.tile(shape, dtype, name=name, tag=TAKES_OVER.get(name, name), align_bytes=64)
+
+        offsets = keep.tile([P, E * C // LIST_COLUMN], U16, name="offsets")
+        xw = kept([P, T], U32, "xw")
+        xs = kept([P, T], U8, "xs")
+        sc_raw = kept([P, E, N], U8, "sc_raw")
+        wb0_raw = [kept([P, PACK, N // 2], F32, "wb0_raw%d" % u) for u in range(2)]
+        wb_raw = {e: kept([P, PACK, N], F32, "wb_raw%d" % e) for e in range(1, E)}
+        wa_raw = {e0: kept([P, e1 - e0, H], I32, "wa_raw%d" % e0) for e0, e1 in WA_GROUPS}
+        w_raw = {e0: kept([P, e1 - e0, 2 * N], U8, "w_raw%d" % e0) for e0, e1 in W_GROUPS}
+        y_words = kept([P, E * C], U32, "y_words")
+        y_scales = kept([P, E * C], U8, "y_scales")
 
         nc.gpsimd.memset(xs[:].bitcast(I32), 0)
         nc.gpsimd.memset(sc_raw[:].rearrange("p e n -> p (e n)").bitcast(I32), 0)
@@ -60,35 +68,34 @@ def tile_moe_elr_s_relu_kernel(
         def wb_rows(e):
             return wb[e].rearrange("(p j) n -> p j n", j=PACK)
 
+        def load_wb0(u):
+            nc.sync.dma_start(out=wb0_raw[u][:], in_=wb_rows(0)[:, :, u * (N // 2) : (u + 1) * (N // 2)])
+
+        def load_wb(e):
+            nc.sync.dma_start(out=wb_raw[e][:], in_=wb_rows(e))
+
         def load_wa(e0, e1):
             nc.sync.dma_start(out=wa_raw[e0][:], in_=wa_words[e0:e1, 0].rearrange("e p n d -> p e (n d)").bitcast(I32))
 
         def load_w(e0, e1):
             nc.sync.dma_start(out=w_raw[e0][:].bitcast(I32), in_=w_words[e0:e1, 0].rearrange("e p b -> p e b").bitcast(I32))
 
-        def load_wb_half(e, u):
-            nc.sync.dma_start(out=wb_raw[e, u][:], in_=wb_rows(e)[:, :, u * (N // 2) : (u + 1) * (N // 2)])
-
-        def load_wb(e):
-            nc.sync.dma_start(out=wb_raw[e][:], in_=wb_rows(e))
-
-        def load_scale_row(row, scales, r):
-            by_row = scales[:, 0].rearrange("e (q r) n -> r q e n", r=4)
-            nc.sync.dma_start(out=sc_raw[row + r : P : 32, :, :].bitcast(I32), in_=by_row[r].bitcast(I32))
+        def load_scale_row(first_row, scales, r):
+            by_row = scales[:, 0].rearrange("e (q r) n -> r q e n", r=SCALE_ROWS)
+            nc.sync.dma_start(out=sc_raw[first_row + r : P : 32, :, :].bitcast(I32), in_=by_row[r].bitcast(I32))
 
         nc.sync.dma_start(offsets[:], offs)
         nc.sync.dma_start(out=xw[:].bitcast(I32), in_=x_words[0].rearrange("p t d -> p (t d)").bitcast(I32))
-        xs_rows = x_scales[0].rearrange("(q r) s -> r q s", r=4)
-        load_wb_half(0, 0)
-        for r in range(4):
+        load_wb0(0)
+        xs_rows = x_scales[0].rearrange("(q r) s -> r q s", r=SCALE_ROWS)
+        for r in range(SCALE_ROWS):
             nc.sync.dma_start(out=xs[r:P:32, :].bitcast(I32), in_=xs_rows[r].bitcast(I32))
-        load_wb_half(0, 1)
-        for r in range(4):
+        load_wb0(1)
+        for e in range(1, SCALAR_WB):
+            load_wb(e)
+        for r in range(SCALE_ROWS):
             load_scale_row(WA_ROW, wa_scales, r)
-        load_wb(1)
-        for r in range(4):
             load_scale_row(0, w_scales, r)
-        load_wb(2)
         load_wa(*WA_GROUPS[0])
         load_wa(*WA_GROUPS[1])
         load_w(*W_GROUPS[0])
@@ -99,214 +106,193 @@ def tile_moe_elr_s_relu_kernel(
         load_wa(*WA_GROUPS[3])
         load_wb(5)
 
-        st = {}
+        made = {}
 
-        def gather_words(pair):
-            words = ring.tile([P, 2 * C], U32, name="xg_words", align_bytes=64)
-            nc.vector.tensor_copy(words[:], xw[:].indirect(offsets[:, pair * C // 8 : (pair + 1) * C // 8]))
-            st[pair, "xg_words"] = words
-
-        def gather_scales(pair):
-            scales = ring.tile([P, 2 * C], U8, name="xg_scales", align_bytes=64)
-            nc.vector.tensor_copy(scales[:], xs[:].indirect(offsets[:, pair * C // 8 : (pair + 1) * C // 8]))
-            st[pair, "xg_scales"] = scales
+        def gather(table, dtype, what, e0, e1):
+            slots = ring.tile([P, (e1 - e0) * C], dtype, name=what, align_bytes=64, bufs=len(PAIRS))
+            nc.vector.tensor_copy(slots[:], table[:].indirect(offsets[:, e0 * C // LIST_COLUMN : e1 * C // LIST_COLUMN]))
+            for e in range(e0, e1):
+                made[e, what] = slots[:, (e - e0) * C : (e - e0 + 1) * C]
 
         def deal_wa(e0, e1):
-            wa_p = keep.tile([P, e1 - e0, H], I32, name="wa_p%d" % e0, align_bytes=64)
+            dealt = kept([P, e1 - e0, H], I32, "wa_dealt%d" % e0)
             nc.vector.tensor_copy(
-                out=wa_p[:].rearrange("p e (t m) -> p e m t", t=PACK),
+                out=dealt[:].rearrange("p e (t m) -> p e m t", t=PACK),
                 in_=wa_raw[e0][:].rearrange("p e (m t) -> p e m t", t=PACK),
             )
             for e in range(e0, e1):
-                st[e, "wa"] = wa_p[:, e - e0, :]
+                made[e, "wa"] = dealt[:, e - e0, :]
 
         def deal_w(e0, e1):
-            w_p = keep.tile([P, e1 - e0, 2 * N], U8, name="w_p%d" % e0, align_bytes=64)
+            dealt = kept([P, e1 - e0, 2 * N], U8, "w_dealt%d" % e0)
             nc.vector.tensor_copy(
-                out=w_p[:].bitcast(U16).rearrange("p e (t m) -> p e t m", t=PACK),
+                out=dealt[:].bitcast(U16).rearrange("p e (t m) -> p e t m", t=PACK),
                 in_=w_raw[e0][:].bitcast(U16).rearrange("p e (m t) -> p e t m", t=PACK),
             )
             for e in range(e0, e1):
-                st[e, "w"] = w_p[:, e - e0, :]
+                made[e, "w"] = dealt[:, e - e0, :]
 
         def deal_scales(e0, e1):
-            sc_p = keep.tile([P, e1 - e0, N], U8, name="sc_p%d" % e0, tag="wa_raw0" if e0 else "sc_p0", align_bytes=64)
+            dealt = kept([P, e1 - e0, N], U8, "sc_dealt%d" % e0)
             nc.vector.tensor_copy(
-                out=sc_p[:].rearrange("p e (t m) -> p e t m", t=PACK),
+                out=dealt[:].rearrange("p e (t m) -> p e t m", t=PACK),
                 in_=sc_raw[:, e0:e1, :].rearrange("p e (m t) -> p e t m", t=PACK),
             )
             for e in range(e0, e1):
-                st[e, "sc"] = sc_p[:, e - e0, :]
+                made[e, "scales"] = dealt[:, e - e0, :]
 
         def round_wb(e):
-            wb_bf = ring.tile([P, PACK, P, PACK], BF16, name="wb_bf", align_bytes=64)
-            on_scalar = [(e, u) not in VECTOR_HALVES for u in range(2)]
-            if e >= SPLIT_LOADS and on_scalar[0] == on_scalar[1]:
-                parts = [(wb_bf[:], wb_raw[e][:], on_scalar[0])]
+            wb_bf = ring.tile([P, PACK, P, PACK], BF16, name="wb_bf", align_bytes=64, bufs=WB_AHEAD)
+            if e == 0:
+                parts = [(wb_bf[:, :, u * (P // 2) : (u + 1) * (P // 2), :], wb0_raw[u]) for u in range(2)]
             else:
-                parts = []
-                for u in range(2):
-                    raw = wb_raw[e, u][:] if e < SPLIT_LOADS else wb_raw[e][:, :, u * (N // 2) : (u + 1) * (N // 2)]
-                    parts.append((wb_bf[:, :, u * 64 : (u + 1) * 64, :], raw, on_scalar[u]))
-            for dst, raw, scalar in parts:
-                dst = dst.rearrange("p t m j -> p m j t")
-                src = raw.rearrange("p j (m t) -> p m j t", t=PACK)
-                if scalar:
-                    nc.scalar.copy(out=dst, in_=src)
-                else:
-                    nc.vector.tensor_copy(out=dst, in_=src)
-            st[e, "wb_bf"] = wb_bf
+                parts = [(wb_bf[:], wb_raw[e])]
+            copy = nc.scalar.copy if e < SCALAR_WB else nc.vector.tensor_copy
+            for rounded, raw in parts:
+                copy(out=rounded.rearrange("p t m j -> p m j t"), in_=raw[:].rearrange("p j (m t) -> p m j t", t=PACK))
+            made[e, "wb_bf"] = wb_bf
 
         def quant_wb(e):
-            words = ring.tile([P, N], U32, name="wb_words", align_bytes=64, bufs=E)
+            words = kept([P, N], U32, "wb_words%d" % e)
             scales = ring.tile([P, N], U8, name="wb_scales", align_bytes=64, bufs=E)
             nc.vector.quantize_mx(
-                out=words[:].bitcast(FP8X4), scales=scales[:], in_=st[e, "wb_bf"][:].rearrange("p t m j -> p (t m j)")
+                out=words[:].bitcast(FP8X4), scales=scales[:], in_=made[e, "wb_bf"][:].rearrange("p t m j -> p (t m j)")
             )
-            st[e, "wbq"] = (words, scales)
+            made[e, "wb_mx"] = (words, scales)
 
         def hidden(e):
-            xg_w, xg_s = st[e // 2, "xg_words"], st[e // 2, "xg_scales"]
             h_bf = ring.tile([P, C, PACK], BF16, name="h_bf", align_bytes=64, bufs=E)
             for u in range(C // HALF):
-                cols = slice((e % 2) * C + u * HALF, (e % 2) * C + (u + 1) * HALF)
-                bank = psum.tile([P, PACK, HALF], F32, name="h_bank", bufs=4)
+                slots = slice(u * HALF, (u + 1) * HALF)
+                bank = psum.tile([P, PACK, HALF], F32, name="h_bank")
                 for t in range(PACK):
-                    m = slice(t * P, (t + 1) * P)
+                    places = slice(t * P, (t + 1) * P)
                     nc.tensor.matmul_mx(
                         out=bank[:, t, :],
-                        lhsT=st[e, "wa"][:, m].bitcast(FP8X4),
-                        lhsT_scale=st[e, "sc"][WA_ROW:P, m],
-                        rhs=xg_w[:, cols].bitcast(FP8X4),
-                        rhs_scale=xg_s[:, cols],
+                        lhsT=made[e, "wa"][:, places].bitcast(FP8X4),
+                        lhsT_scale=made[e, "scales"][WA_ROW:P, places],
+                        rhs=made[e, "x_words"][:, slots].bitcast(FP8X4),
+                        rhs_scale=made[e, "x_scales"][:, slots],
                         start=True,
                         stop=True,
                     )
-                nc.scalar.activation(
-                    out=h_bf[:, u * HALF : (u + 1) * HALF, :], in_=bank[:].rearrange("p t s -> p s t"), func=RELU
-                )
-            st[e, "h_bf"] = h_bf
+                nc.scalar.activation(out=h_bf[:, slots, :], in_=bank[:].rearrange("p t s -> p s t"), func=RELU)
+            made[e, "h_bf"] = h_bf
 
         def quant_h(e):
             words = ring.tile([P, C], U32, name="h_words", align_bytes=64, bufs=E)
             scales = ring.tile([P, C], U8, name="h_scales", align_bytes=64, bufs=E)
             nc.vector.quantize_mx(
-                out=words[:].bitcast(FP8X4), scales=scales[:], in_=st[e, "h_bf"][:].rearrange("p s t -> p (s t)")
+                out=words[:].bitcast(FP8X4), scales=scales[:], in_=made[e, "h_bf"][:].rearrange("p s t -> p (s t)")
             )
-            st[e, "hq"] = (words, scales)
+            made[e, "h_mx"] = (words, scales)
 
         rows_out = out_0.rearrange("(p t) s -> p t s", t=PACK)
         words_out = out_1[0].rearrange("p s d -> p (s d)")
+        y_group = {e: (e0, e1) for e0, e1 in Y_GROUPS for e in range(e0, e1)}
 
-        out_group = {e: (e0, e1) for e0, e1 in OUT_GROUPS for e in range(e0, e1)}
+        def vector_slots(e0, e1):
+            return (e1 - e0) * C if (e0, e1) == VECTOR_ALONE else (e1 - e0) * C // 2
 
         def result(e):
-            xg_w, xg_s = st[e // 2, "xg_words"], st[e // 2, "xg_scales"]
-            wb_w, wb_s = st[e, "wbq"]
-            h_w, h_s = st[e, "hq"]
-            e0, e1 = out_group[e]
+            wb_w, wb_s = made[e, "wb_mx"]
+            h_w, h_s = made[e, "h_mx"]
+            e0, e1 = y_group[e]
             if e == e0:
-                st[e0, "y"] = keep.tile([P, PACK, (e1 - e0) * C], F32, name="y%d" % e0, align_bytes=64)
-                st[e0, "y_bf"] = keep.tile([P, (e1 - e0) * C, PACK], BF16, name="y_bf%d" % e0, align_bytes=64)
-            y, y_bf = st[e0, "y"], st[e0, "y_bf"]
-            halves = range(C // HALF)
-            banks = [psum.tile([P, PACK, HALF], F32, name="y_bank", bufs=4) for u in halves]
+                made[e0, "y"] = kept([P, PACK, (e1 - e0) * C], F32, "y%d" % e0)
+                made[e0, "y_bf"] = kept([P, (e1 - e0) * C, PACK], BF16, "y_bf%d" % e0)
+            y, y_bf = made[e0, "y"], made[e0, "y_bf"]
+            halves = [slice(u * HALF, (u + 1) * HALF) for u in range(C // HALF)]
+            banks = [psum.tile([P, PACK, HALF], F32, name="y_bank") for slots in halves]
             for t in range(PACK):
-                m = slice(t * P, (t + 1) * P)
-                for u in halves:
-                    cols = slice((e % 2) * C + u * HALF, (e % 2) * C + (u + 1) * HALF)
+                places = slice(t * P, (t + 1) * P)
+                for bank, slots in zip(banks, halves):
                     nc.tensor.matmul_mx(
-                        out=banks[u][:, t, :],
-                        lhsT=st[e, "w"][:, 2 * t * P : 2 * (t + 1) * P].bitcast(FP4X4),
-                        lhsT_scale=st[e, "sc"][:, m],
-                        rhs=xg_w[:, cols].bitcast(FP8X4),
-                        rhs_scale=xg_s[:, cols],
+                        out=bank[:, t, :],
+                        lhsT=made[e, "w"][:, 2 * t * P : 2 * (t + 1) * P].bitcast(FP4X4),
+                        lhsT_scale=made[e, "scales"][:, places],
+                        rhs=made[e, "x_words"][:, slots].bitcast(FP8X4),
+                        rhs_scale=made[e, "x_scales"][:, slots],
                         start=True,
                         stop=False,
                     )
-                for u in halves:
-                    own = slice(u * HALF, (u + 1) * HALF)
+                for bank, slots in zip(banks, halves):
                     nc.tensor.matmul_mx(
-                        out=banks[u][:, t, :],
-                        lhsT=wb_w[:, m].bitcast(FP8X4),
-                        lhsT_scale=wb_s[:, m],
-                        rhs=h_w[:, own].bitcast(FP8X4),
-                        rhs_scale=h_s[:, own],
+                        out=bank[:, t, :],
+                        lhsT=wb_w[:, places].bitcast(FP8X4),
+                        lhsT_scale=wb_s[:, places],
+                        rhs=h_w[:, slots].bitcast(FP8X4),
+                        rhs_scale=h_s[:, slots],
                         start=False,
                         stop=True,
                     )
-            for u in halves:
-                place = slice((e - e0) * C + u * HALF, (e - e0) * C + (u + 1) * HALF)
-                if e < E - 1:
-                    nc.scalar.copy(out=y[:, :, place], in_=banks[u][:])
-                else:
-                    nc.scalar.copy(out=y_bf[:, place, :], in_=banks[u][:].rearrange("p t s -> p s t"))
-                    if u == 0:
-                        nc.vector.tensor_copy(out=y[:, :, place], in_=banks[u][:])
-                    else:
-                        nc.scalar.copy(out=y[:, :, place], in_=banks[u][:])
-                    nc.sync.dma_start(out=rows_out[:, :, e * C + u * HALF : e * C + (u + 1) * HALF], in_=y[:, :, place])
-            if e < E - 1:
+            for bank, slots in zip(banks, halves):
+                in_group = slice((e - e0) * C + slots.start, (e - e0) * C + slots.stop)
+                nc.scalar.copy(out=y[:, :, in_group], in_=bank[:])
+                if in_group.start >= vector_slots(e0, e1):
+                    nc.scalar.copy(out=y_bf[:, in_group, :], in_=bank[:].rearrange("p t s -> p s t"))
+            if e == 1:
+                nc.sync.dma_start(out=rows_out[:, :, : 2 * C], in_=y[:])
+            elif e > 1:
                 nc.sync.dma_start(out=rows_out[:, :, e * C : (e + 1) * C], in_=y[:, :, (e - e0) * C : (e - e0 + 1) * C])
 
-        def round_y(e0):
+        def round_y(e0, e1):
+            share = slice(0, vector_slots(e0, e1))
             nc.vector.tensor_copy(
-                out=st[e0, "y_bf"][:].rearrange("p (c i) t -> p c t i", i=4),
-                in_=st[e0, "y"][:].rearrange("p t (c i) -> p c t i", i=4),
+                out=made[e0, "y_bf"][:, share, :].rearrange("p (c i) t -> p c t i", i=4),
+                in_=made[e0, "y"][:, :, share].rearrange("p t (c i) -> p c t i", i=4),
             )
 
         def quant_y(e0, e1):
-            width = HALF if e0 == E - 1 else (e1 - e0) * C
-            for c0 in range(0, (e1 - e0) * C, width):
-                cols = slice(e0 * C + c0, e0 * C + c0 + width)
-                nc.vector.quantize_mx(
-                    out=y_words[:, cols].bitcast(FP8X4),
-                    scales=y_scales[:, cols],
-                    in_=st[e0, "y_bf"][:, c0 : c0 + width, :].rearrange("p s t -> p (s t)"),
-                )
+            slots = slice(e0 * C, e1 * C)
+            nc.vector.quantize_mx(
+                out=y_words[:, slots].bitcast(FP8X4),
+                scales=y_scales[:, slots],
+                in_=made[e0, "y_bf"][:].rearrange("p s t -> p (s t)"),
+            )
             if e1 % 2 == 0:
-                cols = slice((e1 - 2) * C, e1 * C)
-                nc.sync.dma_start(out=words_out[:, 4 * cols.start : 4 * cols.stop].bitcast(I32), in_=y_words[:, cols].bitcast(I32))
+                first = (e1 - 2) * C
+                nc.sync.dma_start(
+                    out=words_out[:, PACK * first : PACK * e1 * C].bitcast(I32), in_=y_words[:, first : e1 * C].bitcast(I32)
+                )
 
-        wa_group, w_group, sc_group = dict(WA_GROUPS), dict(W_GROUPS), dict(SC_GROUPS)
-
-        for pair in range(E // 2):
-            gather_words(pair)
-        for pair in range(E // 2):
-            gather_scales(pair)
-        group_end = {e1 - 1: e0 for e0, e1 in OUT_GROUPS[:-1]}
+        wa_group, w_group, pair = dict(WA_GROUPS), dict(W_GROUPS), dict(PAIRS)
 
         def first_layer(e):
             if e in wa_group:
                 deal_wa(e, wa_group[e])
-            if e in sc_group:
-                deal_scales(e, sc_group[e])
+            if e in pair:
+                deal_scales(e, pair[e])
             hidden(e)
 
-        def operands(e):
+        def result_operands(e):
             if e in w_group:
                 deal_w(e, w_group[e])
             quant_wb(e)
             quant_h(e)
 
+        for e0, e1 in PAIRS:
+            gather(xw, U32, "x_words", e0, e1)
+        for e0, e1 in PAIRS:
+            gather(xs, U8, "x_scales", e0, e1)
         for e in range(WB_AHEAD):
             round_wb(e)
         for e in range(H_AHEAD):
             first_layer(e)
-        operands(0)
+        result_operands(0)
         for e in range(E):
             if e + H_AHEAD < E:
                 first_layer(e + H_AHEAD)
             result(e)
             if e + 1 < E:
-                operands(e + 1)
+                result_operands(e + 1)
             if e + WB_AHEAD < E:
                 round_wb(e + WB_AHEAD)
-            if e - 1 in group_end:
-                quant_y(group_end[e - 1], e)
-            if e in group_end:
-                round_y(group_end[e])
-        quant_y(E - 1, E)
-        by_row = out_2[0].rearrange("(q r) s -> r q s", r=4)
-        for r in range(4):
-            nc.scalar.dma_start(out=by_row[r].bitcast(I32), in_=y_scales[r:P:32, :].bitcast(I32))
+            if e >= 1 and y_group[e - 1][1] == e:
+                quant_y(*y_group[e - 1])
+            if y_group[e][1] == e + 1:
+                round_y(*y_group[e])
+        quant_y(*Y_GROUPS[-1])
+        scales_out = out_2[0].rearrange("(q r) s -> r q s", r=SCALE_ROWS)
+        for r in range(SCALE_ROWS):
+            nc.scalar.dma_start(out=scales_out[r].bitcast(I32), in_=y_scales[r:P:32, :].bitcast(I32))

@@ -22,20 +22,20 @@ LIST_COLUMN = 16
 SCALE_ROWS = 4
 WA_ROW = 4
 
-SCALAR_WB = 3
-H_AHEAD = 2
-WB_AHEAD = 3
-
-PAIRS = [(e, e + 2) for e in range(0, E, 2)]
-WA_GROUPS = [(0, 1), (1, 3), (3, 5), (5, 6)]
-W_GROUPS = [(0, 2), (2, 6)]
-Y_GROUPS = [(0, 2), (2, 4), (4, 5), (5, 6)]
-VECTOR_ALONE = (2, 4)
+PAIRS = [(0, 2), (2, 4), (4, 6)]
+H_GROUPS = PAIRS
+Y_GROUPS = [(0, 2), (2, 3), (3, 5), (5, 6)]
+STORE_GROUPS = [(0, 2), (2, 3), (3, 4), (4, 5), (5, 6)]
+WORD_GROUPS = [(0, 2), (2, 5), (5, 6)]
+BANK_PAIRS = 4
 
 TAKES_OVER = {
-    "sc_dealt2": "wa_raw0",
-    "sc_dealt4": "wa_raw3",
-    "wb_words2": "w_raw0",
+    "sc_dealt4": "xs",
+    "h_words2": "wb_raw1",
+    "h_words4": "wb_raw3",
+    "y_words0": "wb_bf3",
+    "y_bf3": "wb_raw5",
+    "y_words2": "wb_bf5",
 }
 
 
@@ -45,8 +45,7 @@ def tile_moe_elr_s_relu_kernel(
     nc = tc.nc
     with ExitStack() as ctx:
         keep = ctx.enter_context(tc.tile_pool(name="keep", bufs=1))
-        ring = ctx.enter_context(tc.tile_pool(name="ring", bufs=1))
-        psum = ctx.enter_context(tc.psum_pool(name="psum", bufs=4))
+        psum = ctx.enter_context(tc.psum_pool(name="psum", bufs=1))
 
         def kept(shape, dtype, name):
             return keep.tile(shape, dtype, name=name, tag=TAKES_OVER.get(name, name), align_bytes=64)
@@ -55,244 +54,290 @@ def tile_moe_elr_s_relu_kernel(
         xw = kept([P, T], U32, "xw")
         xs = kept([P, T], U8, "xs")
         sc_raw = kept([P, E, N], U8, "sc_raw")
-        wb0_raw = [kept([P, PACK, N // 2], F32, "wb0_raw%d" % u) for u in range(2)]
-        wb_raw = {e: kept([P, PACK, N], F32, "wb_raw%d" % e) for e in range(1, E)}
-        wa_raw = {e0: kept([P, e1 - e0, H], I32, "wa_raw%d" % e0) for e0, e1 in WA_GROUPS}
-        w_raw = {e0: kept([P, e1 - e0, 2 * N], U8, "w_raw%d" % e0) for e0, e1 in W_GROUPS}
-        y_words = kept([P, E * C], U32, "y_words")
-        y_scales = kept([P, E * C], U8, "y_scales")
-
-        nc.gpsimd.memset(xs[:].bitcast(I32), 0)
-        nc.gpsimd.memset(sc_raw[:].rearrange("p e n -> p (e n)").bitcast(I32), 0)
-
-        def wb_rows(e):
-            return wb[e].rearrange("(p j) n -> p j n", j=PACK)
-
-        def load_wb0(u):
-            nc.sync.dma_start(out=wb0_raw[u][:], in_=wb_rows(0)[:, :, u * (N // 2) : (u + 1) * (N // 2)])
-
-        def load_wb(e):
-            nc.sync.dma_start(out=wb_raw[e][:], in_=wb_rows(e))
-
-        def load_wa(e0, e1):
-            nc.sync.dma_start(out=wa_raw[e0][:], in_=wa_words[e0:e1, 0].rearrange("e p n d -> p e (n d)").bitcast(I32))
-
-        def load_w(e0, e1):
-            nc.sync.dma_start(out=w_raw[e0][:].bitcast(I32), in_=w_words[e0:e1, 0].rearrange("e p b -> p e b").bitcast(I32))
-
-        def load_scale_row(first_row, scales, r):
-            by_row = scales[:, 0].rearrange("e (q r) n -> r q e n", r=SCALE_ROWS)
-            nc.sync.dma_start(out=sc_raw[first_row + r : P : 32, :, :].bitcast(I32), in_=by_row[r].bitcast(I32))
-
-        nc.sync.dma_start(offsets[:], offs)
-        nc.sync.dma_start(out=xw[:].bitcast(I32), in_=x_words[0].rearrange("p t d -> p (t d)").bitcast(I32))
-        load_wb0(0)
-        xs_rows = x_scales[0].rearrange("(q r) s -> r q s", r=SCALE_ROWS)
-        for r in range(SCALE_ROWS):
-            nc.sync.dma_start(out=xs[r:P:32, :].bitcast(I32), in_=xs_rows[r].bitcast(I32))
-        load_wb0(1)
-        for e in range(1, SCALAR_WB):
-            load_wb(e)
-        for r in range(SCALE_ROWS):
-            load_scale_row(WA_ROW, wa_scales, r)
-            load_scale_row(0, w_scales, r)
-        load_wa(*WA_GROUPS[0])
-        load_wa(*WA_GROUPS[1])
-        load_w(*W_GROUPS[0])
-        load_wb(3)
-        load_w(*W_GROUPS[1])
-        load_wa(*WA_GROUPS[2])
-        load_wb(4)
-        load_wa(*WA_GROUPS[3])
-        load_wb(5)
-
         made = {}
 
+        def load_x_words():
+            nc.sync.dma_start(out=xw[:].bitcast(I32), in_=x_words[0].rearrange("p t d -> p (t d)").bitcast(I32))
+
+        def load_x_scales():
+            by_row = x_scales[0].rearrange("(q r) s -> r q s", r=SCALE_ROWS)
+            for r in range(SCALE_ROWS):
+                nc.sync.dma_start(out=xs[r:P:32, :].bitcast(I32), in_=by_row[r].bitcast(I32))
+
+        def load_weight_scales():
+            for r in range(SCALE_ROWS):
+                for first_row, scales in ((WA_ROW, wa_scales), (0, w_scales)):
+                    by_row = scales[:, 0].rearrange("e (q r) n -> r q e n", r=SCALE_ROWS)
+                    nc.sync.dma_start(out=sc_raw[first_row + r : P : 32, :, :].bitcast(I32), in_=by_row[r].bitcast(I32))
+
+        def load_wb(e):
+            raw = kept([P, PACK, N], F32, "wb_raw%d" % e)
+            nc.sync.dma_start(out=raw[:], in_=wb[e].rearrange("(p j) n -> p j n", j=PACK))
+            made[e, "wb_raw"] = raw
+
+        def load_wa(e0, e1):
+            raw = kept([P, e1 - e0, H], U32, "wa_raw%d" % e0)
+            nc.sync.dma_start(out=raw[:].bitcast(I32), in_=wa_words[e0:e1, 0].rearrange("e p n d -> p e (n d)").bitcast(I32))
+            for e in range(e0, e1):
+                made[e, "wa_raw"] = (raw, e0)
+
+        def load_w(e0, e1):
+            raw = kept([P, e1 - e0, 2 * N], U8, "w_raw%d" % e0)
+            nc.sync.dma_start(out=raw[:].bitcast(I32), in_=w_words[e0:e1, 0].rearrange("e p b -> p e b").bitcast(I32))
+            made[e0, "w_raw"] = raw
+
         def gather(table, dtype, what, e0, e1):
-            slots = ring.tile([P, (e1 - e0) * C], dtype, name=what, align_bytes=64, bufs=len(PAIRS))
+            slots = kept([P, (e1 - e0) * C], dtype, "%s%d" % (what, e0))
             nc.vector.tensor_copy(slots[:], table[:].indirect(offsets[:, e0 * C // LIST_COLUMN : e1 * C // LIST_COLUMN]))
             for e in range(e0, e1):
                 made[e, what] = slots[:, (e - e0) * C : (e - e0 + 1) * C]
 
-        def deal_wa(e0, e1):
-            dealt = kept([P, e1 - e0, H], I32, "wa_dealt%d" % e0)
-            nc.vector.tensor_copy(
+        def deal_wa(copy, e0, e1):
+            raw, first = made[e0, "wa_raw"]
+            dealt = kept([P, e1 - e0, H], U32, "wa_dealt%d" % e0)
+            copy(
                 out=dealt[:].rearrange("p e (t m) -> p e m t", t=PACK),
-                in_=wa_raw[e0][:].rearrange("p e (m t) -> p e m t", t=PACK),
+                in_=raw[:, e0 - first : e1 - first, :].rearrange("p e (m t) -> p e m t", t=PACK),
             )
             for e in range(e0, e1):
                 made[e, "wa"] = dealt[:, e - e0, :]
 
-        def deal_w(e0, e1):
+        def deal_w(copy, e0, e1):
             dealt = kept([P, e1 - e0, 2 * N], U8, "w_dealt%d" % e0)
-            nc.vector.tensor_copy(
+            copy(
                 out=dealt[:].bitcast(U16).rearrange("p e (t m) -> p e t m", t=PACK),
-                in_=w_raw[e0][:].bitcast(U16).rearrange("p e (m t) -> p e t m", t=PACK),
+                in_=made[e0, "w_raw"][:].bitcast(U16).rearrange("p e (m t) -> p e t m", t=PACK),
             )
             for e in range(e0, e1):
                 made[e, "w"] = dealt[:, e - e0, :]
 
-        def deal_scales(e0, e1):
+        def deal_scales(copy, e0, e1):
             dealt = kept([P, e1 - e0, N], U8, "sc_dealt%d" % e0)
-            nc.vector.tensor_copy(
+            copy(
                 out=dealt[:].rearrange("p e (t m) -> p e t m", t=PACK),
                 in_=sc_raw[:, e0:e1, :].rearrange("p e (m t) -> p e t m", t=PACK),
             )
             for e in range(e0, e1):
                 made[e, "scales"] = dealt[:, e - e0, :]
 
-        def round_wb(e):
-            wb_bf = ring.tile([P, PACK, P, PACK], BF16, name="wb_bf", align_bytes=64, bufs=WB_AHEAD)
-            if e == 0:
-                parts = [(wb_bf[:, :, u * (P // 2) : (u + 1) * (P // 2), :], wb0_raw[u]) for u in range(2)]
-            else:
-                parts = [(wb_bf[:], wb_raw[e])]
-            copy = nc.scalar.copy if e < SCALAR_WB else nc.vector.tensor_copy
-            for rounded, raw in parts:
-                copy(out=rounded.rearrange("p t m j -> p m j t"), in_=raw[:].rearrange("p j (m t) -> p m j t", t=PACK))
+        def round_wb(copy, e):
+            wb_bf = kept([P, PACK, P, PACK], BF16, "wb_bf%d" % e)
+            copy(out=wb_bf[:].rearrange("p t m j -> p m j t"), in_=made[e, "wb_raw"][:].rearrange("p j (m t) -> p m j t", t=PACK))
             made[e, "wb_bf"] = wb_bf
 
         def quant_wb(e):
             words = kept([P, N], U32, "wb_words%d" % e)
-            scales = ring.tile([P, N], U8, name="wb_scales", align_bytes=64, bufs=E)
+            scales = kept([P, N], U8, "wb_scales%d" % e)
             nc.vector.quantize_mx(
                 out=words[:].bitcast(FP8X4), scales=scales[:], in_=made[e, "wb_bf"][:].rearrange("p t m j -> p (t m j)")
             )
             made[e, "wb_mx"] = (words, scales)
 
+        halves = [slice(u * HALF, (u + 1) * HALF) for u in range(C // HALF)]
+        places = [slice(t * P, (t + 1) * P) for t in range(PACK)]
+
         def hidden(e):
-            h_bf = ring.tile([P, C, PACK], BF16, name="h_bf", align_bytes=64, bufs=E)
-            for u in range(C // HALF):
-                slots = slice(u * HALF, (u + 1) * HALF)
-                bank = psum.tile([P, PACK, HALF], F32, name="h_bank")
+            e0, e1 = h_group[e]
+            if e == e0:
+                made[e0, "h_bf"] = kept([P, (e1 - e0) * C, PACK], BF16, "h_bf%d" % e0)
+            for u, slots in enumerate(halves):
+                bank = psum.tile([P, PACK, HALF], F32, name="bank%d_%d" % (e % BANK_PAIRS, u))
                 for t in range(PACK):
-                    places = slice(t * P, (t + 1) * P)
                     nc.tensor.matmul_mx(
                         out=bank[:, t, :],
-                        lhsT=made[e, "wa"][:, places].bitcast(FP8X4),
-                        lhsT_scale=made[e, "scales"][WA_ROW:P, places],
+                        lhsT=made[e, "wa"][:, places[t]].bitcast(FP8X4),
+                        lhsT_scale=made[e, "scales"][WA_ROW:P, places[t]],
                         rhs=made[e, "x_words"][:, slots].bitcast(FP8X4),
                         rhs_scale=made[e, "x_scales"][:, slots],
                         start=True,
                         stop=True,
                     )
-                nc.scalar.activation(out=h_bf[:, slots, :], in_=bank[:].rearrange("p t s -> p s t"), func=RELU)
-            made[e, "h_bf"] = h_bf
+                in_group = slice((e - e0) * C + slots.start, (e - e0) * C + slots.stop)
+                nc.scalar.activation(out=made[e0, "h_bf"][:, in_group, :], in_=bank[:].rearrange("p t s -> p s t"), func=RELU)
 
-        def quant_h(e):
-            words = ring.tile([P, C], U32, name="h_words", align_bytes=64, bufs=E)
-            scales = ring.tile([P, C], U8, name="h_scales", align_bytes=64, bufs=E)
+        def quant_h(e0, e1):
+            words = kept([P, (e1 - e0) * C], U32, "h_words%d" % e0)
+            scales = kept([P, (e1 - e0) * C], U8, "h_scales%d" % e0)
             nc.vector.quantize_mx(
-                out=words[:].bitcast(FP8X4), scales=scales[:], in_=made[e, "h_bf"][:].rearrange("p s t -> p (s t)")
+                out=words[:].bitcast(FP8X4), scales=scales[:], in_=made[e0, "h_bf"][:].rearrange("p s t -> p (s t)")
             )
-            made[e, "h_mx"] = (words, scales)
+            for e in range(e0, e1):
+                mine = slice((e - e0) * C, (e - e0 + 1) * C)
+                made[e, "h_mx"] = (words[:, mine], scales[:, mine])
 
         rows_out = out_0.rearrange("(p t) s -> p t s", t=PACK)
         words_out = out_1[0].rearrange("p s d -> p (s d)")
-        y_group = {e: (e0, e1) for e0, e1 in Y_GROUPS for e in range(e0, e1)}
+        h_group = {e: g for g in H_GROUPS for e in range(*g)}
+        y_group = {e: g for g in Y_GROUPS for e in range(*g)}
+        store_group = {e: g for g in STORE_GROUPS for e in range(*g)}
+        word_group = {e: g for g in WORD_GROUPS for e in range(*g)}
+        y_scales = kept([P, E * C], U8, "y_scales")
 
-        def vector_slots(e0, e1):
-            return (e1 - e0) * C if (e0, e1) == VECTOR_ALONE else (e1 - e0) * C // 2
-
-        def result(e):
+        def products(e):
             wb_w, wb_s = made[e, "wb_mx"]
             h_w, h_s = made[e, "h_mx"]
-            e0, e1 = y_group[e]
-            if e == e0:
-                made[e0, "y"] = kept([P, PACK, (e1 - e0) * C], F32, "y%d" % e0)
-                made[e0, "y_bf"] = kept([P, (e1 - e0) * C, PACK], BF16, "y_bf%d" % e0)
-            y, y_bf = made[e0, "y"], made[e0, "y_bf"]
-            halves = [slice(u * HALF, (u + 1) * HALF) for u in range(C // HALF)]
-            banks = [psum.tile([P, PACK, HALF], F32, name="y_bank") for slots in halves]
-            for t in range(PACK):
-                places = slice(t * P, (t + 1) * P)
-                for bank, slots in zip(banks, halves):
+            banks = [psum.tile([P, PACK, HALF], F32, name="bank%d_%d" % ((e + 2) % BANK_PAIRS, u)) for u in range(len(halves))]
+            for bank, slots in zip(banks, halves):
+                for t in range(PACK):
                     nc.tensor.matmul_mx(
                         out=bank[:, t, :],
                         lhsT=made[e, "w"][:, 2 * t * P : 2 * (t + 1) * P].bitcast(FP4X4),
-                        lhsT_scale=made[e, "scales"][:, places],
+                        lhsT_scale=made[e, "scales"][:, places[t]],
                         rhs=made[e, "x_words"][:, slots].bitcast(FP8X4),
                         rhs_scale=made[e, "x_scales"][:, slots],
-                        start=True,
+                        start=t == 0,
                         stop=False,
                     )
-                for bank, slots in zip(banks, halves):
+            for bank, slots in zip(banks, halves):
+                for t in range(PACK):
                     nc.tensor.matmul_mx(
                         out=bank[:, t, :],
-                        lhsT=wb_w[:, places].bitcast(FP8X4),
-                        lhsT_scale=wb_s[:, places],
+                        lhsT=wb_w[:, places[t]].bitcast(FP8X4),
+                        lhsT_scale=wb_s[:, places[t]],
                         rhs=h_w[:, slots].bitcast(FP8X4),
                         rhs_scale=h_s[:, slots],
                         start=False,
-                        stop=True,
+                        stop=t == PACK - 1,
                     )
-            for bank, slots in zip(banks, halves):
-                in_group = slice((e - e0) * C + slots.start, (e - e0) * C + slots.stop)
-                nc.scalar.copy(out=y[:, :, in_group], in_=bank[:])
-                if in_group.start >= vector_slots(e0, e1):
-                    nc.scalar.copy(out=y_bf[:, in_group, :], in_=bank[:].rearrange("p t s -> p s t"))
-            if e == 1:
-                nc.sync.dma_start(out=rows_out[:, :, : 2 * C], in_=y[:])
-            elif e > 1:
-                nc.sync.dma_start(out=rows_out[:, :, e * C : (e + 1) * C], in_=y[:, :, (e - e0) * C : (e - e0 + 1) * C])
+            made[e, "banks"] = banks
+            if e == store_group[e][0]:
+                made[e, "y"] = kept([P, PACK, (store_group[e][1] - e) * C], F32, "y%d" % e)
+            if e == y_group[e][0]:
+                made[e, "y_bf"] = kept([P, (y_group[e][1] - e) * C, PACK], BF16, "y_bf%d" % e)
 
-        def round_y(e0, e1):
-            share = slice(0, vector_slots(e0, e1))
+        def y_slots(group, what, e, u0, u1):
+            first = group[e][0]
+            return made[first, what], slice((e - first) * C + u0 * HALF, (e - first) * C + u1 * HALF)
+
+        def empty(e, u):
+            y, slots = y_slots(store_group, "y", e, u, u + 1)
+            nc.scalar.copy(out=y[:, :, slots], in_=made[e, "banks"][u][:])
+
+        def round_bank(copy, e, u):
+            y_bf, slots = y_slots(y_group, "y_bf", e, u, u + 1)
+            copy(out=y_bf[:, slots, :], in_=made[e, "banks"][u][:].rearrange("p t s -> p s t"))
+
+        def round_y(e, u0, u1):
+            y, slots = y_slots(store_group, "y", e, u0, u1)
+            y_bf, in_group = y_slots(y_group, "y_bf", e, u0, u1)
             nc.vector.tensor_copy(
-                out=made[e0, "y_bf"][:, share, :].rearrange("p (c i) t -> p c t i", i=4),
-                in_=made[e0, "y"][:, :, share].rearrange("p t (c i) -> p c t i", i=4),
+                out=y_bf[:, in_group, :].rearrange("p (c i) t -> p c t i", i=4),
+                in_=y[:, :, slots].rearrange("p t (c i) -> p c t i", i=4),
             )
+
+        def store_y(e0, e1):
+            nc.sync.dma_start(out=rows_out[:, :, e0 * C : e1 * C], in_=made[e0, "y"][:])
 
         def quant_y(e0, e1):
-            slots = slice(e0 * C, e1 * C)
+            first, last = word_group[e0]
+            if e0 == first:
+                made[first, "y_words"] = kept([P, (last - first) * C], U32, "y_words%d" % first)
+            words = made[first, "y_words"]
             nc.vector.quantize_mx(
-                out=y_words[:, slots].bitcast(FP8X4),
-                scales=y_scales[:, slots],
+                out=words[:, (e0 - first) * C : (e1 - first) * C].bitcast(FP8X4),
+                scales=y_scales[:, e0 * C : e1 * C],
                 in_=made[e0, "y_bf"][:].rearrange("p s t -> p (s t)"),
             )
-            if e1 % 2 == 0:
-                first = (e1 - 2) * C
-                nc.sync.dma_start(
-                    out=words_out[:, PACK * first : PACK * e1 * C].bitcast(I32), in_=y_words[:, first : e1 * C].bitcast(I32)
-                )
+            if e1 == last:
+                nc.sync.dma_start(out=words_out[:, PACK * first * C : PACK * last * C].bitcast(I32), in_=words[:].bitcast(I32))
 
-        wa_group, w_group, pair = dict(WA_GROUPS), dict(W_GROUPS), dict(PAIRS)
+        def store_scales():
+            scales_out = out_2[0].rearrange("(q r) s -> r q s", r=SCALE_ROWS)
+            for r in range(SCALE_ROWS):
+                nc.scalar.dma_start(out=scales_out[r].bitcast(I32), in_=y_scales[r:P:32, :].bitcast(I32))
 
-        def first_layer(e):
-            if e in wa_group:
-                deal_wa(e, wa_group[e])
-            if e in pair:
-                deal_scales(e, pair[e])
-            hidden(e)
+        on_vector, on_scalar, on_gpsimd = nc.vector.tensor_copy, nc.scalar.copy, nc.gpsimd.tensor_copy
 
-        def result_operands(e):
-            if e in w_group:
-                deal_w(e, w_group[e])
-            quant_wb(e)
-            quant_h(e)
+        nc.vector.memset(sc_raw[:].rearrange("p e n -> p (e n)").bitcast(I32), 0)
+        nc.vector.memset(xs[:].bitcast(I32), 0)
 
-        for e0, e1 in PAIRS:
-            gather(xw, U32, "x_words", e0, e1)
-        for e0, e1 in PAIRS:
-            gather(xs, U8, "x_scales", e0, e1)
-        for e in range(WB_AHEAD):
-            round_wb(e)
-        for e in range(H_AHEAD):
-            first_layer(e)
-        result_operands(0)
-        for e in range(E):
-            if e + H_AHEAD < E:
-                first_layer(e + H_AHEAD)
-            result(e)
-            if e + 1 < E:
-                result_operands(e + 1)
-            if e + WB_AHEAD < E:
-                round_wb(e + WB_AHEAD)
-            if e >= 1 and y_group[e - 1][1] == e:
-                quant_y(*y_group[e - 1])
-            if y_group[e][1] == e + 1:
-                round_y(*y_group[e])
-        quant_y(*Y_GROUPS[-1])
-        scales_out = out_2[0].rearrange("(q r) s -> r q s", r=SCALE_ROWS)
-        for r in range(SCALE_ROWS):
-            nc.scalar.dma_start(out=scales_out[r].bitcast(I32), in_=y_scales[r:P:32, :].bitcast(I32))
+        nc.sync.dma_start(offsets[:], offs)
+        load_x_words()
+        load_weight_scales()
+        load_x_scales()
+        load_wa(0, 2)
+        load_wa(2, 4)
+        load_wb(0)
+        load_w(0, 2)
+        load_wb(1)
+        load_wa(4, 6)
+        load_wb(2)
+        load_w(2, 6)
+        load_wb(3)
+        load_wb(4)
+        load_wb(5)
+        gather(xw, U32, "x_words", 0, 2)
+        gather(xw, U32, "x_words", 2, 4)
+        gather(xw, U32, "x_words", 4, 6)
+        gather(xs, U8, "x_scales", 0, 2)
+        gather(xs, U8, "x_scales", 2, 4)
+        gather(xs, U8, "x_scales", 4, 6)
+        deal_scales(on_gpsimd, 0, 2)
+        deal_scales(on_gpsimd, 2, 4)
+        deal_wa(on_scalar, 0, 1)
+        deal_wa(on_scalar, 1, 2)
+        hidden(0)
+        deal_wa(on_scalar, 2, 4)
+        hidden(1)
+        deal_scales(on_vector, 4, 6)
+        round_wb(on_vector, 0)
+        deal_w(on_vector, 0, 2)
+        quant_wb(0)
+        quant_h(0, 2)
+        hidden(2)
+        hidden(3)
+        deal_wa(on_scalar, 4, 6)
+        round_wb(on_vector, 1)
+        quant_h(2, 4)
+        quant_wb(1)
+        products(0)
+        empty(0, 0)
+        empty(0, 1)
+        round_bank(on_scalar, 0, 0)
+        round_bank(on_scalar, 0, 1)
+        hidden(4)
+        hidden(5)
+        round_wb(on_vector, 2)
+        deal_w(on_vector, 2, 6)
+        quant_wb(2)
+        products(1)
+        empty(1, 0)
+        empty(1, 1)
+        store_y(0, 2)
+        round_bank(on_scalar, 1, 0)
+        round_bank(on_scalar, 1, 1)
+        round_wb(on_vector, 3)
+        quant_h(4, 6)
+        quant_wb(3)
+        products(2)
+        empty(2, 0)
+        empty(2, 1)
+        store_y(2, 3)
+        round_bank(on_scalar, 2, 0)
+        round_bank(on_scalar, 2, 1)
+        round_wb(on_vector, 4)
+        quant_y(0, 2)
+        quant_wb(4)
+        products(3)
+        empty(3, 0)
+        empty(3, 1)
+        store_y(3, 4)
+        round_wb(on_vector, 5)
+        quant_wb(5)
+        products(4)
+        empty(4, 0)
+        empty(4, 1)
+        store_y(4, 5)
+        round_bank(on_scalar, 4, 1)
+        products(5)
+        empty(5, 0)
+        empty(5, 1)
+        store_y(5, 6)
+        round_bank(on_scalar, 5, 1)
+        round_y(3, 0, 2)
+        round_y(4, 0, 1)
+        quant_y(2, 3)
+        quant_y(3, 5)
+        round_y(5, 0, 1)
+        quant_y(5, 6)
+        store_scales()

@@ -26,16 +26,17 @@ PAIRS = [(0, 2), (2, 4), (4, 6)]
 H_GROUPS = PAIRS
 Y_GROUPS = [(0, 2), (2, 3), (3, 5), (5, 6)]
 STORE_GROUPS = [(0, 2), (2, 3), (3, 4), (4, 5), (5, 6)]
-WORD_GROUPS = [(0, 2), (2, 5), (5, 6)]
+WORD_GROUPS = [(0, 2), (2, 3), (3, 5), (5, 6)]
 BANK_PAIRS = 4
 
 TAKES_OVER = {
-    "sc_dealt4": "xs",
+    "x_scales4": "sc_raw",
+    "h_words0": "w_raw0",
     "h_words2": "wb_raw1",
     "h_words4": "wb_raw3",
     "y_words0": "wb_bf3",
-    "y_bf3": "wb_raw5",
-    "y_words2": "wb_bf5",
+    "y_words2": "wb_bf4",
+    "y_bf3": "wb_bf5",
 }
 
 
@@ -64,8 +65,8 @@ def tile_moe_elr_s_relu_kernel(
             for r in range(SCALE_ROWS):
                 nc.sync.dma_start(out=xs[r:P:32, :].bitcast(I32), in_=by_row[r].bitcast(I32))
 
-        def load_weight_scales():
-            for r in range(SCALE_ROWS):
+        def load_weight_scales(r0, r1):
+            for r in range(r0, r1):
                 for first_row, scales in ((WA_ROW, wa_scales), (0, w_scales)):
                     by_row = scales[:, 0].rearrange("e (q r) n -> r q e n", r=SCALE_ROWS)
                     nc.sync.dma_start(out=sc_raw[first_row + r : P : 32, :, :].bitcast(I32), in_=by_row[r].bitcast(I32))
@@ -248,19 +249,21 @@ def tile_moe_elr_s_relu_kernel(
 
         on_vector, on_scalar, on_gpsimd = nc.vector.tensor_copy, nc.scalar.copy, nc.gpsimd.tensor_copy
 
-        nc.vector.memset(sc_raw[:].rearrange("p e n -> p (e n)").bitcast(I32), 0)
         nc.vector.memset(xs[:].bitcast(I32), 0)
+        nc.vector.memset(sc_raw[:].rearrange("p e n -> p (e n)").bitcast(I32), 0)
 
         nc.sync.dma_start(offsets[:], offs)
         load_x_words()
-        load_weight_scales()
         load_x_scales()
         load_wa(0, 2)
+        load_weight_scales(0, 2)
         load_wa(2, 4)
+        load_weight_scales(2, 4)
+        load_wa(4, 5)
+        load_wa(5, 6)
         load_wb(0)
         load_w(0, 2)
         load_wb(1)
-        load_wa(4, 6)
         load_wb(2)
         load_w(2, 6)
         load_wb(3)
@@ -271,72 +274,70 @@ def tile_moe_elr_s_relu_kernel(
         gather(xw, U32, "x_words", 4, 6)
         gather(xs, U8, "x_scales", 0, 2)
         gather(xs, U8, "x_scales", 2, 4)
-        gather(xs, U8, "x_scales", 4, 6)
-        deal_scales(on_gpsimd, 0, 2)
-        deal_scales(on_gpsimd, 2, 4)
-        deal_wa(on_scalar, 0, 1)
-        deal_wa(on_scalar, 1, 2)
-        hidden(0)
+        deal_wa(on_scalar, 0, 2)
         deal_wa(on_scalar, 2, 4)
+        deal_scales(on_vector, 0, 2)
+        deal_scales(on_vector, 2, 6)
+        gather(xs, U8, "x_scales", 4, 6)
+        deal_wa(on_scalar, 4, 5)
+        deal_wa(on_scalar, 5, 6)
+        hidden(0)
         hidden(1)
-        deal_scales(on_vector, 4, 6)
         round_wb(on_vector, 0)
         deal_w(on_vector, 0, 2)
         quant_wb(0)
         quant_h(0, 2)
         hidden(2)
         hidden(3)
-        deal_wa(on_scalar, 4, 6)
+        hidden(4)
+        hidden(5)
         round_wb(on_vector, 1)
         quant_h(2, 4)
         quant_wb(1)
         products(0)
         empty(0, 0)
         empty(0, 1)
-        round_bank(on_scalar, 0, 0)
-        round_bank(on_scalar, 0, 1)
-        hidden(4)
-        hidden(5)
-        round_wb(on_vector, 2)
-        deal_w(on_vector, 2, 6)
-        quant_wb(2)
         products(1)
         empty(1, 0)
         empty(1, 1)
         store_y(0, 2)
+        round_bank(on_scalar, 0, 0)
+        round_bank(on_scalar, 0, 1)
         round_bank(on_scalar, 1, 0)
         round_bank(on_scalar, 1, 1)
-        round_wb(on_vector, 3)
-        quant_h(4, 6)
-        quant_wb(3)
+        round_wb(on_vector, 2)
+        deal_w(on_vector, 2, 6)
+        quant_wb(2)
         products(2)
         empty(2, 0)
         empty(2, 1)
         store_y(2, 3)
         round_bank(on_scalar, 2, 0)
         round_bank(on_scalar, 2, 1)
-        round_wb(on_vector, 4)
-        quant_y(0, 2)
-        quant_wb(4)
+        round_wb(on_vector, 3)
+        quant_h(4, 6)
+        quant_wb(3)
         products(3)
         empty(3, 0)
         empty(3, 1)
         store_y(3, 4)
-        round_wb(on_vector, 5)
-        quant_wb(5)
+        round_wb(on_vector, 4)
+        quant_y(0, 2)
+        quant_wb(4)
         products(4)
         empty(4, 0)
         empty(4, 1)
         store_y(4, 5)
-        round_bank(on_scalar, 4, 1)
+        round_wb(on_vector, 5)
+        quant_y(2, 3)
+        quant_wb(5)
         products(5)
         empty(5, 0)
         empty(5, 1)
         store_y(5, 6)
         round_bank(on_scalar, 5, 1)
         round_y(3, 0, 2)
-        round_y(4, 0, 1)
-        quant_y(2, 3)
+        round_y(4, 0, 2)
         quant_y(3, 5)
         round_y(5, 0, 1)
         quant_y(5, 6)

@@ -123,7 +123,10 @@ def tile_moe_elr_s_relu_kernel(
 
         def round_wb(copy, e):
             wb_bf = kept([P, PACK, P, PACK], BF16, "wb_bf%d" % e)
-            copy(out=wb_bf[:].rearrange("p t m j -> p m j t"), in_=made[e, "wb_raw"][:].rearrange("p j (m t) -> p m j t", t=PACK))
+            copy(
+                out=wb_bf[:].rearrange("p t m (a b) -> p m a t b", b=2),
+                in_=made[e, "wb_raw"][:].rearrange("p (a b) (m t) -> p m a t b", b=2, t=PACK),
+            )
             made[e, "wb_bf"] = wb_bf
 
         def quant_wb(e):

@@ -30,14 +30,14 @@ WORD_GROUPS = [(0, 2), (2, 3), (3, 5), (5, 6)]
 BANK_PAIRS = 4
 
 TAKES_OVER = {
-    "x_scales4": "sc_raw",
-    "h_words0": "w_raw0",
-    "h_words2": "wb_raw1",
-    "h_words4": "wb_raw3",
+    "h_bf0": "wa_raw2",
+    "h_words2": "wa_raw4",
+    "h_words4": "wb_words2",
     "y_words0": "wb_bf3",
     "y_words2": "wb_bf4",
     "y_bf3": "wb_bf5",
 }
+PLACES = {"sc_raw": 0, "x_words5": 0, "x_scales4": 2048}
 
 
 def tile_moe_elr_s_relu_kernel(
@@ -46,9 +46,12 @@ def tile_moe_elr_s_relu_kernel(
     nc = tc.nc
     with ExitStack() as ctx:
         keep = ctx.enter_context(tc.tile_pool(name="keep", bufs=1))
+        halved = ctx.enter_context(tc.tile_pool(name="halved", bufs=1))
         psum = ctx.enter_context(tc.psum_pool(name="psum", bufs=1))
 
         def kept(shape, dtype, name):
+            if name in PLACES:
+                return halved.tile(shape, dtype, name=name, offset=PLACES[name], align_bytes=64)
             return keep.tile(shape, dtype, name=name, tag=TAKES_OVER.get(name, name), align_bytes=64)
 
         offsets = keep.tile([P, E * C // LIST_COLUMN], U16, name="offsets")
@@ -260,12 +263,11 @@ def tile_moe_elr_s_relu_kernel(
         load_x_scales()
         load_wa(0, 2)
         load_weight_scales(0, 2)
-        load_wa(2, 4)
-        load_weight_scales(2, 4)
-        load_wa(4, 5)
-        load_wa(5, 6)
-        load_wb(0)
         load_w(0, 2)
+        load_weight_scales(2, 4)
+        load_wa(2, 4)
+        load_wb(0)
+        load_wa(4, 6)
         load_wb(1)
         load_wb(2)
         load_w(2, 6)
@@ -274,38 +276,38 @@ def tile_moe_elr_s_relu_kernel(
         load_wb(5)
         gather(xw, U32, "x_words", 0, 2)
         gather(xw, U32, "x_words", 2, 4)
-        gather(xw, U32, "x_words", 4, 6)
         gather(xs, U8, "x_scales", 0, 2)
         gather(xs, U8, "x_scales", 2, 4)
+        gather(xw, U32, "x_words", 4, 5)
         deal_wa(on_scalar, 0, 2)
+        deal_w(on_scalar, 0, 2)
         deal_wa(on_scalar, 2, 4)
         deal_scales(on_vector, 0, 2)
         deal_scales(on_vector, 2, 6)
+        gather(xw, U32, "x_words", 5, 6)
         gather(xs, U8, "x_scales", 4, 6)
-        deal_wa(on_scalar, 4, 5)
-        deal_wa(on_scalar, 5, 6)
         hidden(0)
         hidden(1)
         round_wb(on_vector, 0)
-        deal_w(on_vector, 0, 2)
-        quant_wb(0)
         quant_h(0, 2)
+        quant_wb(0)
         hidden(2)
         hidden(3)
-        hidden(4)
-        hidden(5)
-        round_wb(on_vector, 1)
-        quant_h(2, 4)
-        quant_wb(1)
+        deal_wa(on_scalar, 4, 6)
         products(0)
         empty(0, 0)
         empty(0, 1)
+        hidden(4)
+        hidden(5)
+        round_bank(on_scalar, 0, 0)
+        round_bank(on_scalar, 0, 1)
+        round_wb(on_vector, 1)
+        quant_h(2, 4)
+        quant_wb(1)
         products(1)
         empty(1, 0)
         empty(1, 1)
         store_y(0, 2)
-        round_bank(on_scalar, 0, 0)
-        round_bank(on_scalar, 0, 1)
         round_bank(on_scalar, 1, 0)
         round_bank(on_scalar, 1, 1)
         round_wb(on_vector, 2)

@@ -24,9 +24,9 @@ WA_ROW = 4
 
 PAIRS = [(0, 2), (2, 4), (4, 6)]
 H_GROUPS = PAIRS
-Y_GROUPS = [(0, 2), (2, 3), (3, 5), (5, 6)]
+Y_GROUPS = [(0, 2), (2, 4), (4, 8), (8, 9), (9, 12)]
 STORE_GROUPS = [(0, 2), (2, 3), (3, 4), (4, 5), (5, 6)]
-WORD_GROUPS = [(0, 2), (2, 3), (3, 5), (5, 6)]
+WORD_GROUPS = [(0, 4), (4, 9), (9, 12)]
 BANK_PAIRS = 4
 
 TAKES_OVER = {
@@ -34,8 +34,10 @@ TAKES_OVER = {
     "h_words2": "wa_raw4",
     "h_words4": "wb_words2",
     "y_words0": "wb_bf3",
-    "y_words2": "wb_bf4",
-    "y_bf3": "wb_bf5",
+    "y_bf0": "wb_raw3",
+    "y_bf2": "wb_raw4",
+    "y_bf4": "wb_bf5",
+    "y_bf9": "wb_words5",
 }
 PLACES = {"sc_raw": 0, "x_words5": 0, "x_scales4": 2048}
 
@@ -175,9 +177,9 @@ def tile_moe_elr_s_relu_kernel(
         rows_out = out_0.rearrange("(p t) s -> p t s", t=PACK)
         words_out = out_1[0].rearrange("p s d -> p (s d)")
         h_group = {e: g for g in H_GROUPS for e in range(*g)}
-        y_group = {e: g for g in Y_GROUPS for e in range(*g)}
+        y_group = {b: g for g in Y_GROUPS for b in range(*g)}
         store_group = {e: g for g in STORE_GROUPS for e in range(*g)}
-        word_group = {e: g for g in WORD_GROUPS for e in range(*g)}
+        word_group = {b: g for g in WORD_GROUPS for b in range(*g)}
         y_scales = kept([P, E * C], U8, "y_scales")
 
         def products(e):
@@ -209,44 +211,48 @@ def tile_moe_elr_s_relu_kernel(
             made[e, "banks"] = banks
             if e == store_group[e][0]:
                 made[e, "y"] = kept([P, PACK, (store_group[e][1] - e) * C], F32, "y%d" % e)
-            if e == y_group[e][0]:
-                made[e, "y_bf"] = kept([P, (y_group[e][1] - e) * C, PACK], BF16, "y_bf%d" % e)
 
-        def y_slots(group, what, e, u0, u1):
-            first = group[e][0]
-            return made[first, what], slice((e - first) * C + u0 * HALF, (e - first) * C + u1 * HALF)
+        def y_slots(e, u0, u1):
+            first = store_group[e][0]
+            return made[first, "y"][:, :, (e - first) * C + u0 * HALF : (e - first) * C + u1 * HALF]
+
+        def y_bf_slots(b0, b1):
+            first, last = y_group[b0]
+            if (first, "y_bf") not in made:
+                made[first, "y_bf"] = kept([P, (last - first) * HALF, PACK], BF16, "y_bf%d" % first)
+            return made[first, "y_bf"][:, (b0 - first) * HALF : (b1 - first) * HALF, :]
 
         def empty(e, u):
-            y, slots = y_slots(store_group, "y", e, u, u + 1)
-            nc.scalar.copy(out=y[:, :, slots], in_=made[e, "banks"][u][:])
+            nc.scalar.copy(out=y_slots(e, u, u + 1), in_=made[e, "banks"][u][:])
 
         def round_bank(copy, e, u):
-            y_bf, slots = y_slots(y_group, "y_bf", e, u, u + 1)
-            copy(out=y_bf[:, slots, :], in_=made[e, "banks"][u][:].rearrange("p t s -> p s t"))
+            copy(out=y_bf_slots(2 * e + u, 2 * e + u + 1), in_=made[e, "banks"][u][:].rearrange("p t s -> p s t"))
 
         def round_y(e, u0, u1):
-            y, slots = y_slots(store_group, "y", e, u0, u1)
-            y_bf, in_group = y_slots(y_group, "y_bf", e, u0, u1)
             nc.vector.tensor_copy(
-                out=y_bf[:, in_group, :].rearrange("p (c i) t -> p c t i", i=4),
-                in_=y[:, :, slots].rearrange("p t (c i) -> p c t i", i=4),
+                out=y_bf_slots(2 * e + u0, 2 * e + u1).rearrange("p (c i) t -> p c t i", i=4),
+                in_=y_slots(e, u0, u1).rearrange("p t (c i) -> p c t i", i=4),
             )
 
         def store_y(e0, e1):
             nc.sync.dma_start(out=rows_out[:, :, e0 * C : e1 * C], in_=made[e0, "y"][:])
 
-        def quant_y(e0, e1):
-            first, last = word_group[e0]
-            if e0 == first:
-                made[first, "y_words"] = kept([P, (last - first) * C], U32, "y_words%d" % first)
+        quantised = []
+
+        def quant_y(b0, b1):
+            first, last = word_group[b0]
+            if (first, "y_words") not in made:
+                made[first, "y_words"] = kept([P, (last - first) * HALF], U32, "y_words%d" % first)
             words = made[first, "y_words"]
             nc.vector.quantize_mx(
-                out=words[:, (e0 - first) * C : (e1 - first) * C].bitcast(FP8X4),
-                scales=y_scales[:, e0 * C : e1 * C],
-                in_=made[e0, "y_bf"][:].rearrange("p s t -> p (s t)"),
+                out=words[:, (b0 - first) * HALF : (b1 - first) * HALF].bitcast(FP8X4),
+                scales=y_scales[:, b0 * HALF : b1 * HALF],
+                in_=y_bf_slots(b0, b1).rearrange("p s t -> p (s t)"),
             )
-            if e1 == last:
-                nc.sync.dma_start(out=words_out[:, PACK * first * C : PACK * last * C].bitcast(I32), in_=words[:].bitcast(I32))
+            quantised.extend(range(b0, b1))
+            if all(b in quantised for b in range(first, last)):
+                slots = slice(PACK * first * HALF, PACK * last * HALF)
+                nc.sync.dma_start(out=words_out[:, slots].bitcast(I32), in_=words[:].bitcast(I32))
 
         def store_scales():
             scales_out = out_2[0].rearrange("(q r) s -> r q s", r=SCALE_ROWS)
@@ -299,8 +305,6 @@ def tile_moe_elr_s_relu_kernel(
         empty(0, 1)
         hidden(4)
         hidden(5)
-        round_bank(on_scalar, 0, 0)
-        round_bank(on_scalar, 0, 1)
         round_wb(on_vector, 1)
         quant_h(2, 4)
         quant_wb(1)
@@ -308,8 +312,6 @@ def tile_moe_elr_s_relu_kernel(
         empty(1, 0)
         empty(1, 1)
         store_y(0, 2)
-        round_bank(on_scalar, 1, 0)
-        round_bank(on_scalar, 1, 1)
         round_wb(on_vector, 2)
         deal_w(on_vector, 2, 6)
         quant_wb(2)
@@ -317,11 +319,11 @@ def tile_moe_elr_s_relu_kernel(
         empty(2, 0)
         empty(2, 1)
         store_y(2, 3)
-        round_bank(on_scalar, 2, 0)
-        round_bank(on_scalar, 2, 1)
         round_wb(on_vector, 3)
         quant_h(4, 6)
         quant_wb(3)
+        round_bank(on_scalar, 0, 0)
+        round_bank(on_scalar, 0, 1)
         products(3)
         empty(3, 0)
         empty(3, 1)
@@ -329,21 +331,26 @@ def tile_moe_elr_s_relu_kernel(
         round_wb(on_vector, 4)
         quant_y(0, 2)
         quant_wb(4)
+        round_bank(on_scalar, 1, 0)
+        round_bank(on_scalar, 1, 1)
         products(4)
         empty(4, 0)
         empty(4, 1)
         store_y(4, 5)
+        round_bank(on_scalar, 4, 0)
         round_wb(on_vector, 5)
-        quant_y(2, 3)
+        quant_y(2, 4)
         quant_wb(5)
         products(5)
         empty(5, 0)
         empty(5, 1)
         store_y(5, 6)
+        round_bank(on_scalar, 4, 1)
         round_bank(on_scalar, 5, 1)
+        round_y(2, 0, 2)
         round_y(3, 0, 2)
-        round_y(4, 0, 2)
-        quant_y(3, 5)
+        quant_y(8, 9)
+        quant_y(4, 8)
         round_y(5, 0, 1)
-        quant_y(5, 6)
+        quant_y(9, 12)
         store_scales()

@@ -25,7 +25,7 @@ WA_ROW = 4
 PAIRS = [(0, 2), (2, 4), (4, 6)]
 H_GROUPS = PAIRS
 Y_GROUPS = [(0, 2), (2, 4), (4, 8), (8, 9), (9, 12)]
-STORE_GROUPS = [(0, 2), (2, 3), (3, 4), (4, 5), (5, 6)]
+STORE_GROUPS = [(0, 3), (3, 4), (4, 5), (5, 6)]
 WORD_GROUPS = [(0, 4), (4, 9), (9, 12)]
 BANK_PAIRS = 4
 
@@ -311,14 +311,13 @@ def tile_moe_elr_s_relu_kernel(
         products(1)
         empty(1, 0)
         empty(1, 1)
-        store_y(0, 2)
         round_wb(on_vector, 2)
         deal_w(on_vector, 2, 6)
         quant_wb(2)
         products(2)
         empty(2, 0)
         empty(2, 1)
-        store_y(2, 3)
+        store_y(0, 3)
         round_wb(on_vector, 3)
         quant_h(4, 6)
         quant_wb(3)

from contextlib import ExitStack

import concourse.mybir as mybir

T, E, C, H, N = 768, 6, 256, 512, 512
FLOPS = 3 * 2 * 512 * 512 * E * C

F32 = mybir.dt.float32
BF16 = mybir.dt.bfloat16
I32 = mybir.dt.int32
U32 = mybir.dt.uint32
U16 = mybir.dt.uint16
U8 = mybir.dt.uint8
FP8X4 = mybir.dt.float8_e4m3fn_x4
FP4X4 = mybir.dt.float4_e2m1fn_x4
RELU = mybir.ActivationFunctionType.Relu

P = 128
PACK = 4
HALF = 128
LIST_COLUMN = 16
SCALE_ROWS = 4
WA_ROW = 4

PAIRS = [(0, 2), (2, 4), (4, 6)]
H_GROUPS = PAIRS
Y_GROUPS = [(0, 2), (2, 4), (4, 8), (8, 9), (9, 12)]
STORE_GROUPS = [(0, 3), (3, 4), (4, 5), (5, 6)]
WORD_GROUPS = [(0, 4), (4, 9), (9, 12)]
BANK_PAIRS = 4

TAKES_OVER = {
    "h_bf0": "wa_raw2",
    "h_words2": "wa_raw4",
    "h_words4": "wb_words2",
    "y_words0": "wb_bf3",
    "y_bf0": "wb_raw3",
    "y_bf2": "wb_raw4",
    "y_bf4": "wb_bf5",
    "y_bf9": "wb_words5",
}
PLACES = {"sc_raw": 0, "x_words5": 0, "x_scales4": 2048}


def tile_moe_elr_s_relu_kernel(
    tc, x_words, x_scales, w_words, w_scales, wa_words, wa_scales, wb, offs, out_0, out_1, out_2
):
    nc = tc.nc
    with ExitStack() as ctx:
        keep = ctx.enter_context(tc.tile_pool(name="keep", bufs=1))
        halved = ctx.enter_context(tc.tile_pool(name="halved", bufs=1))
        psum = ctx.enter_context(tc.psum_pool(name="psum", bufs=1))

        def kept(shape, dtype, name):
            if name in PLACES:
                return halved.tile(shape, dtype, name=name, offset=PLACES[name], align_bytes=64)
            return keep.tile(shape, dtype, name=name, tag=TAKES_OVER.get(name, name), align_bytes=64)

        offsets = keep.tile([P, E * C // LIST_COLUMN], U16, name="offsets")
        xw = kept([P, T], U32, "xw")
        xs = kept([P, T], U8, "xs")
        sc_raw = kept([P, E, N], U8, "sc_raw")
        made = {}

        def load_x_words():
            nc.sync.dma_start(out=xw[:].bitcast(I32), in_=x_words[0].rearrange("p t d -> p (t d)").bitcast(I32))

        def load_x_scales():
            by_row = x_scales[0].rearrange("(q r) s -> r q s", r=SCALE_ROWS)
            for r in range(SCALE_ROWS):
                nc.sync.dma_start(out=xs[r:P:32, :].bitcast(I32), in_=by_row[r].bitcast(I32))

        def load_weight_scales(r0, r1):
            for r in range(r0, r1):
                for first_row, scales in ((WA_ROW, wa_scales), (0, w_scales)):
                    by_row = scales[:, 0].rearrange("e (q r) n -> r q e n", r=SCALE_ROWS)
                    nc.sync.dma_start(out=sc_raw[first_row + r : P : 32, :, :].bitcast(I32), in_=by_row[r].bitcast(I32))

        def load_wb(e):
            raw = kept([P, PACK, N], F32, "wb_raw%d" % e)
            nc.sync.dma_start(out=raw[:], in_=wb[e].rearrange("(p j) n -> p j n", j=PACK))
            made[e, "wb_raw"] = raw

        def load_wa(e0, e1):
            raw = kept([P, e1 - e0, H], U32, "wa_raw%d" % e0)
            nc.sync.dma_start(out=raw[:].bitcast(I32), in_=wa_words[e0:e1, 0].rearrange("e p n d -> p e (n d)").bitcast(I32))
            for e in range(e0, e1):
                made[e, "wa_raw"] = (raw, e0)

        def load_w(e0, e1):
            raw = kept([P, e1 - e0, 2 * N], U8, "w_raw%d" % e0)
            nc.sync.dma_start(out=raw[:].bitcast(I32), in_=w_words[e0:e1, 0].rearrange("e p b -> p e b").bitcast(I32))
            made[e0, "w_raw"] = raw

        def gather(table, dtype, what, e0, e1):
            slots = kept([P, (e1 - e0) * C], dtype, "%s%d" % (what, e0))
            nc.vector.tensor_copy(slots[:], table[:].indirect(offsets[:, e0 * C // LIST_COLUMN : e1 * C // LIST_COLUMN]))
            for e in range(e0, e1):
                made[e, what] = slots[:, (e - e0) * C : (e - e0 + 1) * C]

        def deal_wa(copy, e0, e1):
            raw, first = made[e0, "wa_raw"]
            dealt = kept([P, e1 - e0, H], U32, "wa_dealt%d" % e0)
            copy(
                out=dealt[:].rearrange("p e (t m) -> p e m t", t=PACK),
                in_=raw[:, e0 - first : e1 - first, :].rearrange("p e (m t) -> p e m t", t=PACK),
            )
            for e in range(e0, e1):
                made[e, "wa"] = dealt[:, e - e0, :]

        def deal_w(copy, e0, e1):
            dealt = kept([P, e1 - e0, 2 * N], U8, "w_dealt%d" % e0)
            copy(
                out=dealt[:].bitcast(U16).rearrange("p e (t m) -> p e t m", t=PACK),
                in_=made[e0, "w_raw"][:].bitcast(U16).rearrange("p e (m t) -> p e t m", t=PACK),
            )
            for e in range(e0, e1):
                made[e, "w"] = dealt[:, e - e0, :]

        def deal_scales(copy, e0, e1):
            dealt = kept([P, e1 - e0, N], U8, "sc_dealt%d" % e0)
            copy(
                out=dealt[:].rearrange("p e (t m) -> p e t m", t=PACK),
                in_=sc_raw[:, e0:e1, :].rearrange("p e (m t) -> p e t m", t=PACK),
            )
            for e in range(e0, e1):
                made[e, "scales"] = dealt[:, e - e0, :]

        def round_wb(copy, e):
            wb_bf = kept([P, PACK, P, PACK], BF16, "wb_bf%d" % e)
            copy(
                out=wb_bf[:].rearrange("p t m (a b) -> p m a t b", b=2),
                in_=made[e, "wb_raw"][:].rearrange("p (a b) (m t) -> p m a t b", b=2, t=PACK),
            )
            made[e, "wb_bf"] = wb_bf

        def quant_wb(e):
            words = kept([P, N], U32, "wb_words%d" % e)
            scales = kept([P, N], U8, "wb_scales%d" % e)
            nc.vector.quantize_mx(
                out=words[:].bitcast(FP8X4), scales=scales[:], in_=made[e, "wb_bf"][:].rearrange("p t m j -> p (t m j)")
            )
            made[e, "wb_mx"] = (words, scales)

        halves = [slice(u * HALF, (u + 1) * HALF) for u in range(C // HALF)]
        places = [slice(t * P, (t + 1) * P) for t in range(PACK)]

        def hidden(e):
            e0, e1 = h_group[e]
            if e == e0:
                made[e0, "h_bf"] = kept([P, (e1 - e0) * C, PACK], BF16, "h_bf%d" % e0)
            for u, slots in enumerate(halves):
                bank = psum.tile([P, PACK, HALF], F32, name="bank%d_%d" % (e % BANK_PAIRS, u))
                for t in range(PACK):
                    nc.tensor.matmul_mx(
                        out=bank[:, t, :],
                        lhsT=made[e, "wa"][:, places[t]].bitcast(FP8X4),
                        lhsT_scale=made[e, "scales"][WA_ROW:P, places[t]],
                        rhs=made[e, "x_words"][:, slots].bitcast(FP8X4),
                        rhs_scale=made[e, "x_scales"][:, slots],
                        start=True,
                        stop=True,
                    )
                in_group = slice((e - e0) * C + slots.start, (e - e0) * C + slots.stop)
                nc.scalar.activation(out=made[e0, "h_bf"][:, in_group, :], in_=bank[:].rearrange("p t s -> p s t"), func=RELU)

        def quant_h(e0, e1):
            words = kept([P, (e1 - e0) * C], U32, "h_words%d" % e0)
            scales = kept([P, (e1 - e0) * C], U8, "h_scales%d" % e0)
            nc.vector.quantize_mx(
                out=words[:].bitcast(FP8X4), scales=scales[:], in_=made[e0, "h_bf"][:].rearrange("p s t -> p (s t)")
            )
            for e in range(e0, e1):
                mine = slice((e - e0) * C, (e - e0 + 1) * C)
                made[e, "h_mx"] = (words[:, mine], scales[:, mine])

        rows_out = out_0.rearrange("(p t) s -> p t s", t=PACK)
        words_out = out_1[0].rearrange("p s d -> p (s d)")
        h_group = {e: g for g in H_GROUPS for e in range(*g)}
        y_group = {b: g for g in Y_GROUPS for b in range(*g)}
        store_group = {e: g for g in STORE_GROUPS for e in range(*g)}
        word_group = {b: g for g in WORD_GROUPS for b in range(*g)}
        y_scales = kept([P, E * C], U8, "y_scales")

        def products(e):
            wb_w, wb_s = made[e, "wb_mx"]
            h_w, h_s = made[e, "h_mx"]
            banks = [psum.tile([P, PACK, HALF], F32, name="bank%d_%d" % ((e + 2) % BANK_PAIRS, u)) for u in range(len(halves))]
            for bank, slots in zip(banks, halves):
                for t in range(PACK):
                    nc.tensor.matmul_mx(
                        out=bank[:, t, :],
                        lhsT=made[e, "w"][:, 2 * t * P : 2 * (t + 1) * P].bitcast(FP4X4),
                        lhsT_scale=made[e, "scales"][:, places[t]],
                        rhs=made[e, "x_words"][:, slots].bitcast(FP8X4),
                        rhs_scale=made[e, "x_scales"][:, slots],
                        start=t == 0,
                        stop=False,
                    )
            for bank, slots in zip(banks, halves):
                for t in range(PACK):
                    nc.tensor.matmul_mx(
                        out=bank[:, t, :],
                        lhsT=wb_w[:, places[t]].bitcast(FP8X4),
                        lhsT_scale=wb_s[:, places[t]],
                        rhs=h_w[:, slots].bitcast(FP8X4),
                        rhs_scale=h_s[:, slots],
                        start=False,
                        stop=t == PACK - 1,
                    )
            made[e, "banks"] = banks
            if e == store_group[e][0]:
                made[e, "y"] = kept([P, PACK, (store_group[e][1] - e) * C], F32, "y%d" % e)

        def y_slots(e, u0, u1):
            first = store_group[e][0]
            return made[first, "y"][:, :, (e - first) * C + u0 * HALF : (e - first) * C + u1 * HALF]

        def y_bf_slots(b0, b1):
            first, last = y_group[b0]
            if (first, "y_bf") not in made:
                made[first, "y_bf"] = kept([P, (last - first) * HALF, PACK], BF16, "y_bf%d" % first)
            return made[first, "y_bf"][:, (b0 - first) * HALF : (b1 - first) * HALF, :]

        def empty(e, u):
            nc.scalar.copy(out=y_slots(e, u, u + 1), in_=made[e, "banks"][u][:])

        def round_bank(copy, e, u):
            copy(out=y_bf_slots(2 * e + u, 2 * e + u + 1), in_=made[e, "banks"][u][:].rearrange("p t s -> p s t"))

        def round_y(e, u0, u1):
            nc.vector.tensor_copy(
                out=y_bf_slots(2 * e + u0, 2 * e + u1).rearrange("p (c i) t -> p c t i", i=4),
                in_=y_slots(e, u0, u1).rearrange("p t (c i) -> p c t i", i=4),
            )

        def store_y(e0, e1):
            nc.sync.dma_start(out=rows_out[:, :, e0 * C : e1 * C], in_=made[e0, "y"][:])

        quantised = []

        def quant_y(b0, b1):
            first, last = word_group[b0]
            if (first, "y_words") not in made:
                made[first, "y_words"] = kept([P, (last - first) * HALF], U32, "y_words%d" % first)
            words = made[first, "y_words"]
            nc.vector.quantize_mx(
                out=words[:, (b0 - first) * HALF : (b1 - first) * HALF].bitcast(FP8X4),
                scales=y_scales[:, b0 * HALF : b1 * HALF],
                in_=y_bf_slots(b0, b1).rearrange("p s t -> p (s t)"),
            )
            quantised.extend(range(b0, b1))
            if all(b in quantised for b in range(first, last)):
                slots = slice(PACK * first * HALF, PACK * last * HALF)
                nc.sync.dma_start(out=words_out[:, slots].bitcast(I32), in_=words[:].bitcast(I32))

        def store_scales():
            scales_out = out_2[0].rearrange("(q r) s -> r q s", r=SCALE_ROWS)
            for r in range(SCALE_ROWS):
                nc.scalar.dma_start(out=scales_out[r].bitcast(I32), in_=y_scales[r:P:32, :].bitcast(I32))

        on_vector, on_scalar, on_gpsimd = nc.vector.tensor_copy, nc.scalar.copy, nc.gpsimd.tensor_copy

        nc.vector.memset(xs[:].bitcast(I32), 0)
        nc.vector.memset(sc_raw[:].rearrange("p e n -> p (e n)").bitcast(I32), 0)

        nc.sync.dma_start(offsets[:], offs)
        load_x_words()
        load_x_scales()
        load_wa(0, 2)
        load_weight_scales(0, 2)
        load_w(0, 2)
        load_weight_scales(2, 4)
        load_wa(2, 4)
        load_wb(0)
        load_wa(4, 6)
        load_wb(1)
        load_wb(2)
        load_w(2, 6)
        load_wb(3)
        load_wb(4)
        load_wb(5)
        gather(xw, U32, "x_words", 0, 2)
        gather(xw, U32, "x_words", 2, 4)
        gather(xs, U8, "x_scales", 0, 2)
        gather(xs, U8, "x_scales", 2, 4)
        gather(xw, U32, "x_words", 4, 5)
        deal_wa(on_scalar, 0, 2)
        deal_w(on_scalar, 0, 2)
        deal_wa(on_scalar, 2, 4)
        deal_scales(on_vector, 0, 2)
        deal_scales(on_vector, 2, 6)
        gather(xw, U32, "x_words", 5, 6)
        gather(xs, U8, "x_scales", 4, 6)
        hidden(0)
        hidden(1)
        round_wb(on_vector, 0)
        quant_h(0, 2)
        quant_wb(0)
        hidden(2)
        hidden(3)
        deal_wa(on_scalar, 4, 6)
        products(0)
        empty(0, 0)
        empty(0, 1)
        hidden(4)
        hidden(5)
        round_wb(on_vector, 1)
        quant_h(2, 4)
        quant_wb(1)
        products(1)
        empty(1, 0)
        empty(1, 1)
        round_wb(on_vector, 2)
        deal_w(on_vector, 2, 6)
        quant_wb(2)
        products(2)
        empty(2, 0)
        empty(2, 1)
        store_y(0, 3)
        round_wb(on_vector, 3)
        quant_h(4, 6)
        quant_wb(3)
        round_bank(on_scalar, 0, 0)
        round_bank(on_scalar, 0, 1)
        products(3)
        empty(3, 0)
        empty(3, 1)
        store_y(3, 4)
        round_wb(on_vector, 4)
        quant_y(0, 2)
        quant_wb(4)
        round_bank(on_scalar, 1, 0)
        round_bank(on_scalar, 1, 1)
        products(4)
        empty(4, 0)
        empty(4, 1)
        store_y(4, 5)
        round_bank(on_scalar, 4, 0)
        round_wb(on_vector, 5)
        quant_y(2, 4)
        quant_wb(5)
        products(5)
        empty(5, 0)
        empty(5, 1)
        store_y(5, 6)
        round_bank(on_scalar, 4, 1)
        round_bank(on_scalar, 5, 1)
        round_y(2, 0, 2)
        round_y(3, 0, 2)
        quant_y(8, 9)
        quant_y(4, 8)
        round_y(5, 0, 1)
        quant_y(9, 12)
        store_scales()
